import numpy as np, ml_dtypes
CORES = [2,3,42,43,82,83,122,123]
N = 8
import mx_ref
BF = ml_dtypes.bfloat16
def gcols(t, e):
    v = np.concatenate([t.reshape(8, 16, -1, 4), np.zeros((8, 16, 1, 4), BF)], axis=2)
    return np.ascontiguousarray(np.stack([v[g][:, e[g]] for g in range(8)])).reshape(128, -1)
def gpick(z, e):
    return np.concatenate([z[16 * g:16 * g + 16][:, e[g]] for g in range(8)])
def tile(rs):
    return np.stack(rs, axis=2).reshape(128, -1).astype(BF)
def pick(q, e):
    c = np.concatenate([q[0].reshape(128, -1, 4), np.zeros((128, 1, 4), np.uint8)], axis=1); s = np.concatenate([q[1], np.ones((16, 1), np.uint8)], axis=1)
    return (np.ascontiguousarray(c[:, e].reshape(128, -1)), np.ascontiguousarray(s[:, e]))
def join(*qs):
    return (np.concatenate([q[0] for q in qs], axis=1), np.concatenate([q[1] for q in qs], axis=1))
def put(q, e, v):
    c, s = q[0].reshape(128, -1, 4).copy(), q[1].copy(); c[:, e] = v[0].reshape(128, -1, 4); s[:, e] = v[1]
    return (c.reshape(128, -1), s)
def pk(c, s):
    return (np.ascontiguousarray(c), mx_ref.live(s))
def emit(q):
    return q[0], q[1]
def packed(v, rng):
    q = [mx_ref.quantize(np.ascontiguousarray(v[r])) for r in range(N)]
    return np.stack([a for a, b in q]), np.stack([mx_ref.plane(b, rng) for a, b in q])
def values_of_codes():
    e, c = np.zeros((128, 128, 4), np.float32), np.zeros((128, 2, 4), np.uint8)
    e[np.arange(128), np.arange(128), 0] = 1
    c[:127, :, 0] = np.arange(256).reshape(2, 128).T[:127]
    return mx_ref.matmul(mx_ref.quantize(e.reshape(128, 512).astype(BF)), (c.reshape(128, 8), np.full((16, 2), 127, np.uint8))).T.reshape(-1).astype(np.float64)
CODE_VALUE, SCALE_VALUE = values_of_codes(), 2.0 ** (np.arange(256) - 127.0)
def decode(q):
    return (CODE_VALUE[q[0]].reshape(16, 8, -1, 4) * SCALE_VALUE[q[1]][:, None, :, None] + 0.0).reshape(128, -1).astype(np.float32)
def f(rng, *shape):
    return mx_ref.flush((rng.standard_normal(shape, dtype=np.float32) * np.exp2(rng.integers(-2, 3, shape[:-1] + (1,)))).astype(BF))
def wide(rng, *shape, cols=0):
    v = rng.standard_normal(shape, dtype=np.float32) * np.exp2(rng.integers(-12, 13, shape)).astype(np.float32)
    if cols: v *= np.repeat(np.exp2(rng.integers(-cols, cols + 1, shape[:-2] + (1, shape[-1] // 4))) * (rng.random(shape[:-2] + (1, shape[-1] // 4)) > 0.0625), 4, axis=-1).astype(np.float32)
    return mx_ref.flush(v.astype(BF))
C, K, R = 256, 64, 3
STEP = [1, 2, 4]
def partner(r, t):
    return r ^ STEP[t]
def basins(s):
    s = s + np.float32(0.0)
    j = np.arange(C)
    o = np.argsort(-s, axis=1, kind="stable")
    w = C - 1 - np.argsort(o, axis=1)
    up = w[:, None, :] > w[:, :, None]
    before, behind = j < j[:, None], j > j[:, None]
    l = np.max(np.where(up & before, j, -1), axis=2)
    r = np.min(np.where(up & behind, j, C), axis=2)
    a = np.where(l < 0, -1, np.min(np.where(before & (j > l[:, :, None]), w[:, None, :], C), axis=2))
    b = np.where(r == C, -1, np.min(np.where(behind & (j < r[:, :, None]), w[:, None, :], C), axis=2))
    other = (a < C) & (b < C) & (w < C - 1)
    q = np.where(other, np.take_along_axis(o, np.where(other, C - 1 - np.maximum(a, b), 0), axis=1), j)
    p = s - np.take_along_axis(s, q, axis=1)
    first = np.where(w == C - 1, 0, np.where(other, 1, 2))
    e = np.sort(np.lexsort((-p, first))[:, :K], axis=1)
    edge = np.full((8, 1), -1)
    beside = np.where(np.concatenate([edge, w[:, :-1]], axis=1) > np.concatenate([w[:, 1:], edge], axis=1), j - 1, j + 1)
    to = np.where(other, np.where(a > b, l, r), beside)
    np.put_along_axis(to, e, e, axis=1)
    for i in range(C.bit_length()): to = np.take_along_axis(to, to, axis=1)
    k = np.zeros((8, C), np.int64)
    np.put_along_axis(k, e, np.tile(np.arange(K), (8, 1)), axis=1)
    return e, np.take_along_axis(q, e, axis=1), to, np.take_along_axis(k, to, axis=1)
def big(v):
    v = v.astype(np.float32)
    v[np.abs(v) < np.float32(2.0 ** -16)] = 0
    return v.astype(BF)
def numbers_of(rng):
    return {"x": big(f(rng, N, 128, 4 * C)), "u": np.array(f(rng, N, 128, 512)), "v": np.array(f(rng, N, 128, 512))}
def weights(rng, w):
    c, p = packed(w, rng)
    return {"wc": c, "ws": p}
def some(rng, keep):
    w = np.array(f(rng, N, 128, 2048)).reshape(N, 128, 4, 8, 16, 4)
    w[:, :, :, :, [i for i in range(16) if i not in keep]] = 0
    return weights(rng, w.reshape(N, 128, 2048))
def unit(rng, keep, a):
    w = np.zeros((N, 128, 4, 128, 4), np.float32)
    i = np.array([i for i in range(128) if i % 16 in keep])
    for b in range(4): w[:, i, b, i, b] = a
    return weights(rng, w.reshape(N, 128, 2048).astype(BF))
def whole(rng, *shape):
    return rng.integers(4, 8, shape) * rng.choice([-1.0, 1.0], shape)
def plant(d, s, c, m, top, k):
    x = d["x"].astype(np.float32).reshape(N, 8, 16, C, 4)
    x[:, :, 0] = 0
    x[:, :, 0, :, 0] = c * m
    u = d["u"].reshape(N, 128, 128, 4)
    u[:, :, ::16] = 0
    for i in range(3): x[:, :, 8 + i] = ((s[..., None] >> np.arange(4 * i, 4 * i + 4)) & 1) * 2.0 ** np.arange(4) * m
    for h in range(0, 128, 16):
        u[:, h, h, 0] = (k * top).astype(np.float32).astype(BF)
        for i in range(3): u[:, h + 8 + i, h] = (k * 16.0 ** i).astype(np.float32).astype(BF)[:, None]
    return {"x": x.reshape(N, 128, 4 * C).astype(BF), "u": u.reshape(N, 128, 512), "v": d["v"]}
def setup_inputs(rng):
    return {**numbers_of(rng), **weights(rng, f(rng, N, 128, 2048))}
def setup_inputs_ties(rng):
    d = numbers_of(rng)
    e = rng.permutation(N)
    x = d["x"].reshape(N, 8, 16, C, 4)
    for r in range(N):
        k = np.zeros(C, int) if r == e[0] else rng.permutation(C) % 3
        a = x[r][:, :8, :3].copy()
        a[:, :, 2] = 0
        x[r][:, :8] = a[:, :, k]
    x[e[1]] = 0
    u = d["u"].reshape(N, 8, 16, 128, 4)
    u[:, :, 8:, ::16] = 0
    return {"x": x.reshape(N, 128, 4 * C), "u": u.reshape(N, 128, 512), "v": d["v"], **some(rng, range(8, 16))}
def setup_inputs_near(rng):
    d = numbers_of(rng)
    m = 2.0 ** -29
    x = np.zeros((N, 8, 16, C, 4), np.float32)
    x[:, :, 1:8] = whole(rng, N, 8, 7, C, 4) * 4 * m
    x[:, :, 11:] = whole(rng, N, 8, 5, C, 4) * m
    d["x"] = x
    j = np.arange(C)
    fall = C // 2 - 1 - j // 2
    fall = fall + 2 * (fall == C // 2 - K - 1) - 2 * (fall == C // 2 - K + 1)
    c, s = np.zeros((N, 8, C)), np.zeros((N, 8, C), np.int64)
    for r in range(N):
        g = rng.permutation(8)
        for i in range(8):
            c[r, i] = np.where(j % 2 == 1, 1.0, -1.0 * (g[i] % 2))
            s[r, i] = np.where(j % 2 == 1, fall if g[i] == 3 else j // 2, 0)
            if g[i] >= 4:
                s[r, i] = rng.integers(0, 256, C)
                c[r, i, 2 * rng.permutation(C // 2)[:2] + 1] = 2.0 ** 30
    k = np.where(rng.permutation(N) < N // 2, 2.0 ** -30, 1.0)
    return {**plant(d, s, c, m, 2.0 ** 23, k), **unit(rng, range(1, 8), 32)}
def setup_inputs_slopes(rng):
    d = numbers_of(rng)
    j = np.arange(C)
    e = np.stack([j, C - 1 - j, np.minimum(j, C - 1 - j), np.abs(j - C // 2), 0 * j, j // 2, j // 8, np.where(j < 2 * K, j % 2 * (C + j), C - 1 - j)])
    s = np.stack([e[rng.permutation(8)] for r in range(N)])
    c = np.where(rng.permutation(N) < N // 2, -1.0, 0.0)[:, None, None] * np.ones((N, 8, C))
    return {**plant(d, s, c, 1.0, 4096.0, np.ones(N)), **some(rng, range(1, 8))}
def setup_inputs_huge(rng):
    d = numbers_of(rng)
    x = 2.0 ** 30 * (0.5 + 0.3 * rng.random((N, 128, C, 4)))
    c = np.tile(np.arange(C) % 2 * 2.0 - 1.0, (N, 1))
    c[rng.permutation(N) < N // 2] = 1
    x *= c[:, None, :, None]
    g = np.stack([rng.permutation(8) % 2 * 2.0 - 1.0 for r in range(N)])
    u = d["u"].reshape(N, 128, 128, 4)
    u[:, :, ::16] = (2.0 ** 30 * (1 - 0.25 * rng.random((N, 128, 8, 4))) * g[:, None, :, None]).astype(np.float32).astype(BF)
    return {"x": x.astype(np.float32).reshape(N, 128, 4 * C).astype(BF), "u": u.reshape(N, 128, 512), "v": d["v"], **unit(rng, range(16), 1)}
def setup_inputs_spread(rng):
    d = setup_inputs(rng)
    d["x"] = big(wide(rng, N, 128, 4 * C, cols=6))
    return d
def check_inputs(d):
    b = []
    for k in ("x", "u", "v"):
        a = np.abs(d[k].astype(np.float32))
        if not (np.isfinite(a).all() and ((a == 0) | (a >= 2.0 ** -30) & (a <= 2.0 ** 30)).all()): b.append("a value of " + k)
    return b
def reference(x, u, v, wc, ws):
    qu = [mx_ref.quantize(u[r]) for r in range(N)]
    lay = [pk(wc[r], ws[r]) for r in range(N)]
    now = [x[r] for r in range(N)]
    ends = [None] * N
    for t in range(R):
        held, place, sent = [], [], []
        for r in range(N):
            q = mx_ref.quantize(now[r])
            held.append(decode(q))
            e, low, ends[r], h = basins(mx_ref.matmul(qu[r], q)[::16])
            place.append(h)
            own = held[r].astype(BF)
            blend = (gcols(own, e).astype(np.float32) + gcols(own, low).astype(np.float32)) * np.float32(0.5)
            sent.append(mx_ref.quantize(blend.astype(BF)))
        for r in range(N):
            came = sent[partner(r, t)]
            made = [np.maximum(mx_ref.matmul(pick(lay[r], np.arange(128 * b, 128 * b + 128)), came), np.float32(0.0)) * np.float32(0.03125) for b in range(4)]
            now[r] = tile([held[r][:, b::4] + gpick(made[b], place[r]) for b in range(4)])
    y, ol = np.zeros((N, 128, C), np.float32), np.zeros((N, 8, C), np.float32)
    oc, osc = np.zeros((N, 128, 4 * C), np.uint8), np.zeros((N, 16, C), np.uint8)
    for r in range(N):
        q = mx_ref.quantize(now[r])
        y[r] = mx_ref.matmul(mx_ref.quantize(v[r]), q)
        ol[r] = ends[r]
        oc[r], osc[r] = emit(q)
    return {"y": y, "ol": ol, "oc": oc, "osc": osc}

@@ -1,0 +1,615 @@
+import numpy as np
+import math
+from concourse.mybir import dt, AluOpType, AxisListType, ActivationFunctionType
+import comms_topo
+
+C, K, R = 256, 64, 3
+STEP = [1, 2, 4]
+F32, B16, I32, U16, U8, MX = "float32", "bfloat16", "int32", "uint16", "uint8", "float8_e4m3fn_x4"
+INIT = float(2 ** 20 + 256)
+LIFT, LIFT2 = float(2 ** 21), 128.0
+BASE = 192.0
+ALL = 66560
+SPAN = C - K + 16
+CYCLE, FIXED, WAKE, NET = 0.83, 0.0, 220.0, 2500.0
+CASES = ((1.0, 190.0, 3500.0), (1.0, 240.0, 2500.0), (1.25, 210.0, 2500.0))
+TRIES = 7000
+ORDERS = {}
+
+_SB = {
+    F32: {"sm": 64, "c8": 8, "Sw": 784, "M": 128, "VV": 128, "PK": 128, "tmV": 256,
+          "tmM": 128, "tmN": 128, "tsV": 256, "tsM": 128, "tsN": 128, "tRL": 128, "tRR": 128, "tNP": 128, "NJ": 128, "nkL": 136,
+          "Gp": 128, "np": 128, "CT": 256, "g128": 128, "s128": 128, "s64": 64, "H": 256, "G3": 640, "lm": 256, "out": 256,
+          "yb": 256},
+    B16: {"X0": 1024, "X1": 1024, "ut": 512, "vt": 512, "et": 520, "et1": 520, "rbt": 512, "zt": 512, "one": 64, "idn": 128, "A": 272, "A2": 272,
+          "du": 256, "pk": 256, "npk": 256, "np2": 256, "ni": 256, "nf": 256, "th": 256, "thB": 256, "hpx": 256, "hp": 128, "FV": 1024, "FE": 512,
+          "UL": 1040, "UR": 1040, "K": 256, "pcw": 272, "ed": 416, "ec": 416, "cn": 416, "Tf": 512, "Th": 2048, "TE": 256, "F": 512,
+          "tsb": 256, "vL": 128, "nW": 256, "vl": 256, "hv": 256, "WM": 384, "WD": 384, "WO": 384, "r": 272},
+    U16: {"su": 64},
+    MX: {"uq0": 128, "uq": 128, "vq": 128, "wq": 512, "eq": 512, "rbq": 128, "zq": 128, "FVq": 256, "FEq": 128, "XQ": 256},
+    U8: {"us0": 128, "us": 128, "vs": 128, "wp": 512, "es": 512, "rbs": 128, "zs": 128, "FVs": 256, "FEs": 128, "XS": 256},
+}
+for _n, _d in (("RL", F32), ("RR", F32), ("NP", B16)):
+    for _h in "01":
+        _SB[_d][_n + _h] = 128
+for _t in range(R):
+    for _n, _d in (("Fq", MX), ("Fs", U8), ("lc", MX), ("ls", U8)):
+        _SB[_d]["%s%d" % (_n, _t)] = 128
+_JOINT = {
+    "kf": (F32, {"iw": 776, "cf": 256, "jc": 128, "col": 256, "cq": 8}),
+    "kb": (B16, {"mk": 256, "sgb": 128, "par": 256, "mkS": 64, "dg": 776, "ng": 144, "mP": 128, "rst": 128, "mkV": 256, "rstV": 256, "dL": 128,
+                 "dL2": 256, "mt": 256, "mu": 256}),
+    "ki": (I32, {"ci": 256, "cj": 256, "c0": 8, "c1": 8, "c2": 8}),
+    "rb": (B16, {"uu": 256, "u2": 256, "bv": 256, "BB2": 256, "nE": 256, "Sg": 256, "pen": 256, "D": 256, "D2": 256}),
+    "l8s": (I32, {"k8": 8, "l8": 8}),
+}
+WIDTH = {n: w for l in _SB.values() for n, w in l.items()}
+TYPE = {n: d for d, l in _SB.items() for n in l}
+PLACE = {}
+SCRATCH = {n: ("sbuf", [128, WIDTH[n]], TYPE[n]) for n in WIDTH}
+for _b, (_d, _l) in _JOINT.items():
+    _o = 0
+    for _n, _w in _l.items():
+        PLACE[_n], WIDTH[_n], TYPE[_n] = (_b, _o), _w, _d
+        _o += (_w + 31) // 32 * 32
+    SCRATCH[_b] = ("sbuf", [128, _o], _d)
+_PS = ("ps0", "ps1", "psr", "pst")
+for _n in _PS:
+    SCRATCH[_n] = ("psum", [128, 2048 if _n == "pst" else 512], F32)
+    TYPE[_n] = F32
+SEMAPHORES = ["qv", "qa", "qt", "qg"] + ["d%d" % i for i in range(48)] + ["arr%d" % t for t in range(R)] + ["snt"]
+
+
+def planner(g, T):
+    eng = {"v": g.vector, "a": g.scalar, "t": g.tensor, "g": g, "s": g.sync}
+    ops, log = [], {}
+
+    def span(v):
+        n, a, b, s = v
+        if n in _PS:
+            return n, a // 512 * 512, (b + 511) // 512 * 512, 1
+        if s < 0:
+            k = (a - b + (-s) - 1) // (-s)
+            return n, a + s * (k - 1), a + 1, -s
+        return n, a, b, s
+
+    def meet(x, y):
+        (_, a, b, s), (_, c, d, r) = x, y
+        if a >= d or c >= b:
+            return False
+        return not (a - c) % math.gcd(s, r)
+
+    def add(q, call, reads, writes, cost, hold=None, sem=None, inc=1, adds=False):
+        i, pre = len(ops), {}
+        for kind, vs in (("r", reads), ("w", writes)):
+            for v in vs:
+                x = span(v)
+                for (y, k2, j) in log.get(x[0], []):
+                    if meet(x, y) and (kind == "w" or k2 == "w" or (x[0] in _PS and ops[j]["q"] != q)):
+                        pre[j] = pre.get(j, False) or not (adds and x[0] in _PS and ops[j]["q"] == q)
+        for kind, vs in (("r", reads), ("w", writes)):
+            for v in vs:
+                x = span(v)
+                l = log.setdefault(x[0], [])
+                if kind == "w" and x[3] == 1:
+                    l[:] = [e for e in l if not (x[1] <= e[0][1] and e[0][2] <= x[2])]
+                l.append((x, kind, i))
+        ops.append({"q": q, "call": call, "pre": pre, "cost": cost, "hold": cost if hold is None else hold, "sem": sem or "q" + q, "inc": inc})
+
+    def best_order():
+        n = len(ops)
+        succ, rank = [[] for _ in range(n)], [0.0] * n
+        for i, o in enumerate(ops):
+            for j, w in o["pre"].items():
+                succ[j].append((i, WAKE if w else 0.0))
+        for i in range(n - 1, -1, -1):
+            rank[i] = ops[i]["cost"] + max([rank[k] + w for k, w in succ[i]], default=0.0)
+        names = sorted({o["q"] for o in ops})
+        qs = [names.index(o["q"]) for o in ops]
+        cost, hold, need = [o["cost"] for o in ops], [o["hold"] for o in ops], [len(o["pre"]) for o in ops]
+
+        def order(rk, patience):
+            left, ready, free, cand = need[:], [0.0] * n, [0.0] * len(names), [[] for _ in names]
+            pick, out, end = [None] * len(names), [], 0.0
+            for i in range(n):
+                if not left[i]:
+                    cand[qs[i]].append(i)
+            while True:
+                best = None
+                for q, l in enumerate(cand):
+                    if not l:
+                        continue
+                    if pick[q] is None:
+                        t = max(free[q], min([ready[i] for i in l])) + patience
+                        top, r = -1, -1e18
+                        for i in l:
+                            if ready[i] <= t and rk[i] > r:
+                                top, r = i, rk[i]
+                        pick[q] = (max(free[q], ready[top]), -r, top)
+                    if best is None or pick[q] < best[0]:
+                        best = (pick[q], q)
+                if best is None:
+                    return end, out
+                (t, _, i), q = best
+                cand[q].remove(i)
+                pick[q] = None
+                out.append(i)
+                free[q] = t + hold[i]
+                done = t + cost[i]
+                end = max(end, done)
+                for k, w in succ[i]:
+                    ready[k] = max(ready[k], done + w)
+                    left[k] -= 1
+                    if not left[k]:
+                        cand[qs[k]].append(k)
+                        pick[qs[k]] = None
+
+        cases = []
+        for f, wake, net in CASES:
+            pre = [[(j, wake if w else 0.0) for j, w in o["pre"].items()] for o in ops]
+            sent = [o["cost"] == NET for o in ops]
+            c = [net if s else x if x > 2000.0 else f * x for s, x in zip(sent, cost)]
+            cases.append((pre, c, [net if s and h else h if x > 2000.0 else f * h for s, x, h in zip(sent, cost, hold)]))
+
+        def judge(out):
+            total = 0.0
+            for pre, c, h in cases:
+                fin, free, end = [0.0] * n, [0.0] * len(names), 0.0
+                for i in out:
+                    q = qs[i]
+                    t = free[q]
+                    for j, w in pre[i]:
+                        x = fin[j] + w
+                        if x > t:
+                            t = x
+                    free[q] = t + h[i]
+                    fin[i] = t = t + c[i]
+                    if t > end:
+                        end = t
+                total += end
+            return total
+
+        rng, at, best, least = np.random.default_rng(0), np.arange(n), None, 1e18
+        for k in range(TRIES):
+            if k < 200:
+                noise, patience = rng.random(n) * (0.0, 100.0, 300.0, 800.0)[k // 4 % 4], (0.0, 20.0, 50.0, 100.0)[k % 4]
+            else:
+                noise, patience = best[2].copy(), best[3] if k % 5 else 10.0 * (k // 5 % 11)
+                some = (np.abs(at - rng.integers(0, n)) < (5, 20, 60, 200)[k % 4]) & (rng.random(n) < (0.6, 0.3, 0.15, 0.1)[k % 4])
+                noise[some] += rng.normal(0.0, (100.0, 300.0, 800.0)[k % 3], int(some.sum()))
+            end, out = order([r + x for r, x in zip(rank, noise.tolist())], patience)
+            if end > least + 500.0:
+                continue
+            least, end = min(least, end), judge(out)
+            if best is None or end <= best[0]:
+                best = (end, out, noise, patience)
+        return best[1]
+
+    def issue():
+        key = str([(o["q"], o["cost"], sorted(o["pre"].items())) for o in ops])
+        if key not in ORDERS:
+            ORDERS[key] = best_order()
+        count, at, known, snap = {}, {}, {q: {} for q in eng}, {}
+        for i in ORDERS[key]:
+            o = ops[i]
+            q, s = o["q"], o["sem"]
+            kn = known.setdefault(q, {})
+            if q in eng:
+                want = {}
+                for j, w in o["pre"].items():
+                    if w:
+                        want[ops[j]["sem"]] = max(want.get(ops[j]["sem"], 0), at[j])
+                for s2, m in sorted(want.items()):
+                    if kn.get(s2, 0) >= m:
+                        continue
+                    eng[q].wait_ge(T.sem[s2], m)
+                    kn[s2] = m
+                    for k, x in snap.get((s2, m), {}).items():
+                        kn[k] = max(kn.get(k, 0), x)
+            count[s] = count.get(s, 0) + o["inc"]
+            at[i] = count[s]
+            if o["call"]:
+                o["call"](eng[q])
+            snap[(s, at[i])] = dict(kn) if q in eng else {}
+        for s in sorted(count):
+            if known["g"].get(s, 0) < count[s]:
+                g.wait_ge(T.sem[s], count[s])
+    return add, issue
+
+
+def rank_program(g, core, T, topo):
+    rank = T.rank_of(core)
+    if rank is None:
+        return
+    OP, AF = AluOpType, ActivationFunctionType
+    add, issue = planner(g, T)
+    nd = [0]
+
+    def V(n, a=None, b=None, s=1):
+        if a is None:
+            return (n, 0, WIDTH[n], 1)
+        return (n, a, b, s)
+
+    def ap(v):
+        n, a, b, s = v
+        if n in PLACE:
+            n, o = PLACE[n]
+            a, b = a + o, b + o
+        if s < 0:
+            return T[n][:, a:(b if b >= 0 else None):s]
+        return T[n][:, a:b:s] if s != 1 else T[n][:, a:b]
+
+    def ind(v, l):
+        return ap(v).indirect(ap(l))
+
+    def sc(x):
+        return ap(x) if isinstance(x, tuple) else x
+
+    def scr(*xs):
+        return [x for x in xs if isinstance(x, tuple)]
+
+    def width(v):
+        return len(range(v[1], v[2], v[3]))
+
+    def short(*vs):
+        return all(TYPE[v[0]] in (B16, U16) for v in vs)
+
+    def do(q, call, reads, writes, cycles, adds=False):
+        add(q, lambda e: call(e).then_inc(T.sem["q" + q], 1), reads, writes, max(64, cycles) * CYCLE + FIXED, adds=adds)
+
+    def dma(q, out, in_, reads, writes):
+        s = "d%d" % nd[0]
+        nd[0] += 1
+        add(q, lambda e: e.dma_start(out, in_).then_inc(T.sem[s], 16), reads, writes, 2501.0, 100.0, s, 16)
+
+    def tt(out, a, b, op, l=None):
+        n = width(out)
+        n = 60 + 1.5 * n if l else n if a[0] in _PS or b[0] in _PS else 2 * n
+        do("v", lambda e: e.tensor_tensor(ap(out), ind(a, l) if l else ap(a), ap(b), op), [a, b] + scr(l), [out], n)
+
+    def half(out, *a):
+        return width(out) * (0.5 if short(out, *a) else 1.0)
+
+    def ts(out, a, s1, s2, op0, op1=None):
+        if op1 is None:
+            do("v", lambda e: e.tensor_scalar(ap(out), ap(a), sc(s1), None, op0), [a] + scr(s1), [out], half(out, a))
+        else:
+            do("v", lambda e: e.tensor_scalar(ap(out), ap(a), sc(s1), sc(s2), op0, op1), [a] + scr(s1, s2), [out], half(out, a))
+
+    def scan(out, d0, d1, init, op0, op1):
+        do("v", lambda e: e.tensor_tensor_scan(ap(out), ap(d0), ap(d1), init, op0, op1), [d0, d1], [out], half(out, d0, d1))
+
+    def copy(out, a):
+        do("v", lambda e: e.tensor_copy(ap(out), ap(a)), [a], [out], half(out, a))
+
+    def fill(v, c):
+        do("v", lambda e: e.memset(ap(v), c), [], [v], half(v))
+
+    def act(out, a, f, bias=0.0, scale=1.0, l=None, acc=None):
+        def call(e):
+            kw = {}
+            if isinstance(bias, tuple) or bias != 0.0:
+                kw["bias"] = sc(bias)
+            if isinstance(scale, tuple) or scale != 1.0:
+                kw["scale"] = sc(scale)
+            if acc:
+                kw["accum_out"] = ap(acc)
+            return e.activation(ap(out), ind(a, l) if l else ap(a), f, **kw)
+        n = width(out)
+        do("a", call, [a] + scr(bias, scale, l), [out] + scr(acc), 78 + 1.5 * n if l else n + (24 if acc else 0))
+
+    def quant(q, s, x):
+        do("v", lambda e: e.quantize_mx(ap(q), ap(s), ap(x)), [x], [q, s], 14 + 0.265 * width(x))
+
+    def mm(out, l, ls, r, rs, start=True, stop=True):
+        do("t", lambda e: e.matmul_mx(ap(out), ap(l), ap(ls), ap(r), ap(rs), start, stop), [l, ls, r, rs], [out], width(r) + 16, not start)
+
+    def iota(v, pat, base, cm):
+        kw = {} if TYPE[v[0]] == I32 else {"allow_small_or_imprecise_dtypes": True}
+        do("g", lambda e: e.iota(ap(v), pat, base, cm, **kw), [], [v], 160 + 2 * width(v))
+
+    def level(n, a, b, c):
+        iota(V(n, a, b), [[0, b - a]], c, 0)
+
+    def select(v, pat, op, base, cm):
+        do("g", lambda e: e.affine_select(ap(v), ap(v), pat, op, 0.0, base, cm), [v], [v], 200 + 2 * width(v))
+
+    def bits(out, a, n):
+        do("v", lambda e: e.tensor_scalar(ap(out), ap(a), n, None, OP.bitwise_and), [a], [out], width(out))
+
+    def dscan(out, src, lift):
+        scan(out, lift, src, 0.0, OP.add, OP.max)
+
+    def less(out, a, b):
+        scan(out, a, b, 0.0, OP.max, OP.subtract)
+
+    LI, EL, QL, NL, HL, UO = V("su", 0, 8), V("su", 8, 12), V("su", 12, 16), V("su", 16, 24), V("su", 24, 40), V("su", 40, 48)
+
+    dma("s", ap(V("X0")), T.x[:, :], [], [V("X0")])
+    dma("a", ap(V("ut")), T.u[:, :], [], [V("ut")])
+    dma("s", ap(V("wq")).bitcast(dt.uint8), T.wc[:, :], [], [V("wq")])
+    dma("a", ap(V("wp")), T.ws[:, :], [], [V("wp")])
+    dma("s", ap(V("vt")), T.v[:, :], [], [V("vt")])
+
+    iota(V("ci"), [[1, 256]], 256, -1)
+    bits(V("cj"), V("ci"), 15)
+    copy(V("cf"), V("cj"))
+    ts(V("mk"), V("cf"), 0.0, None, OP.is_equal)
+    iota(V("c0"), [[16, 8]], 0, 0)
+    copy(UO, V("c0"))
+    for n, w, k, c0, c in (("sgb", 128, 32, 0.0, 1.0), ("par", 256, 2, 0.0, 1.0), ("rst", 128, 16, -4.95e29, 4.95e29), ("rstV", 256, 32, 4.95e29, -4.95e29)):
+        fill(V(n, 0, w), c)
+        fill(V(n, 0, w, k), c0)
+    for a, b in ((0, 8), (264, 520), (776, 784)):
+        fill(V("Sw", a, b), -1e25)
+    for p in range(2):
+        ts(V("mkV", p, 256, 2), V("mk", 0, 128), 0.5, -9.9e29, OP.subtract, OP.mult)
+    ts(V("tmV", 0, 1), V("mkV", 0, 1), -1e25, None, OP.max)
+    ts(V("mP"), V("mk", 0, 128), 0.5, 9.9e29, OP.subtract, OP.mult)
+    for d, n, c in (("dL", 128, LIFT), ("dL2", 256, LIFT2)):
+        ts(V("mt", 0, n), V("mk", 0, n), c, None, OP.mult)
+        ts(V("mu", 0, n), V("mk", 0, n), -1e29, None, OP.mult)
+        copy(V(d, 0, 1), V("mu", 0, 1))
+        tt(V(d, 1, n), V("mu", 1, n), V("mt", 0, n - 1), OP.add)
+    ts(V("mkS"), V("mk", 0, 64), -2.0 ** 20, 2.0 ** 20, OP.mult, OP.add)
+    fill(V("dg"), -65.0)
+    fill(V("dg", 512, 768), -1.0)
+    for k, c in enumerate((0.0, 1.0)):
+        fill(V("WM", k, 384, 3), c)
+    fill(V("WD", 2, 384, 3), 64.0)
+    quant(V("uq0"), V("us0"), V("ut"))
+    do("v", lambda e: e.tensor_copy(T.uq[:, 0:128].bitcast(dt.uint32), T.uq0[:, 0:128].bitcast(dt.uint32).indirect(ap(UO))), [V("uq0"), UO], [V("uq")], 250)
+    act(V("us"), V("us0", 0, 128), AF.Copy, l=UO)
+    fill(V("idn"), 1.0)
+    fill(V("one"), 1.0)
+    fill(V("c8"), 1024.0)
+    select(V("c8"), [[-16, 8]], OP.is_ge, 0, 1)
+    select(V("c8"), [[16, 8]], OP.is_ge, 15, -1)
+    for m in range(8):
+        act(V("rbt", 64 * m, 64 * m + 64), V("one"), AF.Copy, scale=V("c8", m, m + 1))
+    select(V("idn"), [[-1, 128]], OP.is_equal, 0, 1)
+    iota(V("c1"), [[0, 8]], 0, 1)
+    iota(V("jc"), [[2, 128]], 131072, 0)
+    iota(V("ng", 16, 144), [[-1, 128]], 128, 0)
+    iota(V("iw", 0, 256), [[1, 256]], ALL + 256, 0)
+    level("iw", 256, 512, ALL)
+    iota(V("iw", 512, 768), [[1, 256]], ALL + 256, 0)
+    level("iw", 768, 776, ALL)
+    iota(V("col"), [[1, 256]], 0, 0)
+    for n, o in (("et", 4), ("et1", 5)):
+        fill(V(n), 0.0)
+        act(V(n, o, o + 509, 4), V("idn"), AF.Copy)
+    for b in range(4):
+        o = (4, 4, 2, 2)[b]
+        quant(V("eq", 128 * b, 128 * b + 128), V("es", 128 * b, 128 * b + 128), V(("et", "et1")[b % 2], o, o + 512))
+    quant(V("rbq"), V("rbs"), V("rbt"))
+    bits(V("c2"), V("c1"), 15)
+    copy(V("cq"), V("c2"))
+    for m in range(4):
+        ts(V("sm", m, m + 1), V("cq", 0, 1), 16.0 * m + BASE + 0.5, None, OP.add)
+    ts(V("sm", 11, 12), V("cq", 0, 1), 15.0, None, OP.is_lt)
+    ts(V("sm", 8, 9), V("sm", 11, 12), 2.0 * LIFT, 273.0, OP.mult, OP.add)
+    ts(V("sm", 9, 10), V("sm", 11, 12), -LIFT2, -1.0, OP.mult, OP.add)
+    for v, c in ((V("A"), 0.0), (V("nW"), 1.0), (V("UL", 15, 16), 1.0), (V("UR", 1024, 1025), 1.0), (V("nkL", 128, 129), 0.0), (V("ng", 15, 16), 0.0),
+                 (V("pcw", 0, 16), BASE), (V("nE"), 1.0), (V("r", 0, 16), 0.0)):
+        fill(v, c)
+    level("FE", 0, 512, 0)
+    level("g128", 0, 128, 0)
+    level("F", 256, 512, 0)
+    level("zt", 0, 512, 0)
+    quant(V("zq"), V("zs"), V("zt"))
+    for t in range(R):
+        dma("s", T["lc%d" % t][:, 64:128].bitcast(dt.uint8), T.zq[:, 64:128].bitcast(dt.uint8), [V("zq")], [V("lc%d" % t, 64, 128)])
+        dma("s", T["ls%d" % t][:, 64:128], T.zs[:, 64:128], [V("zs")], [V("ls%d" % t, 64, 128)])
+    quant(V("vq"), V("vs"), V("vt"))
+
+    far = [T.cores[rank ^ s] for s in STEP]
+    engs = topo.engines(core, far[1])
+    mask = 0
+    for e in engs:
+        mask |= 1 << e
+
+    def send(t):
+        rid, pid, _ = topo.addr(far[t])
+        arr = T.sem["arr%d" % t]
+
+        def call(e):
+            e.remote_dma(T["lc%d" % t][:, 0:64].bitcast(dt.uint8), T["Fq%d" % t][:, 0:64].bitcast(dt.uint8), arr, T.sem.snt, pid, rid, mask)
+            e.remote_dma(T["ls%d" % t][:, 0:64], T["Fs%d" % t][:, 0:64], arr, T.sem.snt, pid, rid, mask)
+        add("g", call, [V("Fq%d" % t), V("Fs%d" % t)], [], NET, NET, "snt", 2 * len(engs))
+        add("in", None, [V("Fq%d" % t)], [V("lc%d" % t, 0, 64), V("ls%d" % t, 0, 64)], NET, 0.0, "arr%d" % t, 2 * len(engs))
+
+    XQ, XS, P = V("XQ"), V("XS"), V("psr", 0, 128)
+    pc = V("pcw", 16, 272)
+
+    def product(l, ls, X, banks):
+        for h in range(2):
+            q, s = V("XQ", 128 * h, 128 * h + 128), V("XS", 128 * h, 128 * h + 128)
+            quant(q, s, V(X, 512 * h, 512 * h + 512))
+            for n in banks:
+                n, o = ("ps%d" % h, 0) if n == "ps" else (n, 512 * h)
+                mm(V(n, o, o + 128), V(l), V(ls), q, s)
+
+    def ranks(tiles):
+        for i, h in enumerate(tiles):
+            x, q, s = (V("FE"), V("FEq"), V("FEs")) if h == 2 else (V("FV", 512 * h, 512 * h + 512), V("FVq", 128 * h, 128 * h + 128),
+                                                                    V("FVs", 128 * h, 128 * h + 128))
+            quant(q, s, x)
+            mm(P, V("rbq"), V("rbs"), q, s, i == 0, i == len(tiles) - 1)
+
+    def slot(m, a=0, b=128):
+        o = 512 * (m // 4) + m % 4
+        return V("FV", o + 4 * a, 512 * (m // 4) + 4 * b, 4)
+
+    def climb(n, d, o, init, w):
+        for m in range(7, -1, -1):
+            k = 16 * m + 15 + (m == 0)
+            scan(V("%s%d" % (n, m // 4), 80 + 16 * (m % 4) - k, 80 + 16 * (m % 4)), V("UL", 144 * m + 31 - k, 144 * m + 31),
+                 V(d, o + 16 * m + 15 - k, o + 16 * m + 15), init, OP.mult, OP.max)
+        for h in range(2):
+            dscan(V(w, 64 * h, 64 * h + 64), V("%s%d" % (n, h), 64, 128), V("dL", 0, 64))
+
+    for t in range(R):
+        product("uq", "us", "X%d" % (t % 2), ("ps", "pst"))
+        for h in range(2):
+            act(V("Sw", 128 * h + 8, 128 * h + 136), V("pst", 512 * h, 512 * h + 128), AF.Copy)
+        for b in range(4):
+            mm(V("pst", 512 * b, 512 * b + 256), V("eq", 128 * b, 128 * b + 128), V("es", 128 * b, 128 * b + 128), XQ, XS)
+        for h in range(2):
+            S, o, e = "ps%d" % h, 128 * h, 128 - h
+            tt(V("tmV", o + 1, o + 1 + e), V(S, 0, e), V("mkV", o + 1, o + 1 + e), OP.max)
+            tt(V("VV", o // 2, o // 2 + 64), V(S, 0, 128, 2), V("Sw", o + 7, o + 135, 2), OP.min)
+            scan(V("tsV", o, o + 128), V("rstV", o, o + 128), V("tmV", o, o + 128), 0.0, OP.max, OP.min)
+            tt(V("M", o // 2, o // 2 + 64), V(S, 0, 128, 2), V("Sw", o + 9, o + 137, 2), OP.max)
+            tt(V("A", o, o + 128), V(S, 0, 128), V("Sw", o + 7, o + 135), OP.is_gt)
+        for h in range(2):
+            o, e = 128 * h, 128 - h
+            tt(V("nW", o + 1, o + 1 + e), V("ps%d" % h, 0, e), V("Sw", o + 10, o + 10 + e), OP.is_ge)
+        for m in range(8):
+            s = V("tsV", 32 * m + 31, 32 * m + 32)
+            if m < 2:
+                ts(slot(m), V("VV"), s, None, OP.is_lt)
+            else:
+                act(slot(m), V("VV"), AF.Sign, bias=s, scale=-1.0)
+        scan(V("tmM"), V("M"), V("mP"), -4e29, OP.max, OP.min)
+        scan(V("tsM"), V("rst"), V("tmM"), 0.0, OP.min, OP.max)
+        dma("s", T.Sw[:, 520:776], T.Sw[:, 8:264], [V("Sw", 8, 264)], [V("Sw", 520, 776)])
+        scan(V("NJ"), V("A", 0, 256, 2), V("jc"), 0.0, OP.max, OP.subtract)
+        for m in range(8):
+            s = V("tsM", 16 * m + 15, 16 * m + 16)
+            act(V("UL", 16 + 128 * m, 16 + 128 * m + 16 * m + 16), V("M", 0, 16 * m + 16), AF.Sign, bias=s, scale=-1.0)
+            r = V("UR", 128 * m + 16 * m, 128 * m + 128)
+            if m < 4:
+                ts(r, V("M", 16 * m, 128), s, None, OP.is_le)
+            else:
+                act(r, V("M", 16 * m, 128), AF.Sign, bias=s, scale=-1.0)
+                act(r, r, AF.Sign, bias=0.5)
+        ranks((0, 1))
+        tt(V("nkL", 0, 128), P, V("NJ"), OP.subtract)
+        act(V("A2", 0, 257), V("A", 0, 257), AF.Copy, bias=2.0)
+        less(V("du"), V("A2", 0, 256), V("A2", 1, 257))
+        scan(V("hpx"), V("par"), V("du"), 0.0, OP.mult, OP.max)
+        ts(V("hp"), V("hpx", 1, 256, 2), 2e29, -1e27, OP.mult, OP.add)
+        scan(V("PK"), V("hp"), V("M"), 0.0, OP.add, OP.min)
+        act(V("pk"), V("du"), AF.Relu)
+        act(V("npk"), V("pk"), AF.Copy, bias=1.0, scale=-1.0)
+        act(V("np2"), V("pk"), AF.Copy, bias=132096.0, scale=-65536.0)
+        for b in range(4):
+            act(V("Th", 512 * b, 512 * b + 256), V("pst", 512 * b, 512 * b + 256), AF.Copy, scale=0.5)
+            dma("s", T.Th[:, 512 * b + 256:512 * b + 512], T.Th[:, 512 * b:512 * b + 256], [V("Th", 512 * b, 512 * b + 256)],
+                [V("Th", 512 * b + 256, 512 * b + 512)])
+        climb("RL", "nkL", 1, INIT, "tRL")
+        for m in range(8):
+            a, e = 16 * m, 127 + m // 7
+            scan(V("RR%d" % (m // 4), e - 1 - a + a % 64, a % 64 - 1, -1), V("UR", 128 * m + e, 128 * m + a, -1), V("nkL", e, a, -1), INIT, OP.mult,
+                 OP.max)
+        for h in range(2):
+            dscan(V("tRR", 64 * h, 64 * h + 64), V("RR%d" % h, 0, 64), V("dL", 0, 64))
+        ts(V("sm", 40, 48), V("tRR", 15, 128, 16), 512.0, None, OP.add)
+        tt(V("k8"), V("tRL", 15, 128, 16), V("sm", 40, 48), OP.min)
+        bits(V("l8"), V("k8"), 1023)
+        copy(LI, V("l8"))
+        tt(V("np"), V("Sw", 8, 784), V("PK"), OP.subtract, l=LI)
+        scan(V("tmN"), V("np"), V("mP"), -4e29, OP.max, OP.min)
+        scan(V("tsN", 127, -1, -1), V("rst"), V("tmN", 127, -1, -1), 0.0, OP.min, OP.max)
+        for m in range(8):
+            s = V("tsN", 16 * m, 16 * m + 1)
+            if m < 5:
+                act(slot(m, 16 * m, 128), V("np", 16 * m, 128), AF.Relu, bias=s, scale=-1.0)
+                act(slot(m, 16 * m, 128), slot(m, 16 * m, 128), AF.Sign)
+            else:
+                ts(slot(m, 16 * m, 128), V("np", 16 * m, 128), s, None, OP.is_lt)
+            if m:
+                ts(slot(m, 0, 16 * m), V("np", 0, 16 * m), s, None, OP.is_le)
+        tt(V("FE", 0, 512, 4), V("np"), V("tsN"), OP.is_equal)
+        ranks((2, 1, 0))
+        act(V("Gp"), V("iw"), AF.Copy, l=LI)
+        act(V("WD", 1, 384, 3), V("dg"), AF.Copy, l=LI)
+        scan(V("ni"), V("npk"), V("npk"), 0.0, OP.add, OP.max)
+        ts(V("sm", 10, 11), V("ni", 255, 256), -float(2 ** 20), 192.0 * 2 ** 20, OP.mult, OP.add)
+        ts(V("sm", 12, 13), V("sm", 10, 11), float(ALL), float(ALL), OP.add, OP.min)
+        act(V("nf"), V("ni"), AF.Relu, bias=V("sm", 10, 11), scale=float(2 ** 20))
+        scan(V("th"), V("nf"), V("np2"), 0.0, OP.max, OP.min)
+        ts(V("thB"), V("th"), float(ALL), 2.0 ** -10, OP.max, OP.mult)
+        climb("NP", "ng", 16, 200.0, "tNP")
+        for p in range(2):
+            tt(V("K", p, 256, 2), P, V("th", p, 256, 2), OP.is_ge)
+        scan(pc, V("K"), V("K"), BASE, OP.add, OP.max)
+        for m in range(4):
+            w, o = V("pcw", 16 + 16 * m, 16 + 16 * m + SPAN), SPAN * (m % 2)
+            if m < 2:
+                ts(V("ec", o, o + SPAN), w, V("sm", m, m + 1), None, OP.is_le)
+                scan(V("cn", o, o + SPAN), V("ec", o, o + SPAN), V("ec", o, o + SPAN), 16.0 * m, OP.add, OP.max)
+            else:
+                act(V("ed", o, o + SPAN), w, AF.Sign, bias=V("sm", m, m + 1), scale=-1.0, acc=V("sm", 16 + m, 17 + m))
+                ts(V("su", 8 + m, 9 + m), V("sm", 16 + m, 17 + m), 0.5, SPAN / 2.0 + 16.0 * m, OP.mult, OP.add)
+        copy(V("su", 8, 10), V("cn", SPAN - 1, 2 * SPAN, SPAN))
+        for b in range(2):
+            act(V("Tf", 256 * b, 256 * b + 256), V("pst", 512 * b, 512 * b + 256), AF.Copy)
+        for b in range(4):
+            act(V("TE", 64 * b, 64 * b + 64), V("Th", 512 * b, 512 * b + 256), AF.Copy, l=EL)
+        for p in range(2):
+            less(V("CT", p, 256, 2), V("np2", p, 256, 2), V("Gp"))
+        ts(V("g128", 31, 128, 32), EL, -1.0, None, OP.mult)
+        tt(V("g128", 0, 128, 2), V("CT"), V("mkS"), OP.add, l=EL)
+        scan(V("s128"), V("sgb"), V("g128"), 0.0, OP.mult, OP.min)
+        ts(QL, V("s128", 31, 128, 32), -1.0, None, OP.mult)
+        for b in range(4):
+            tt(V("F", b, 256, 4), V("Th", 512 * b, 512 * b + 512), V("TE", 64 * b, 64 * b + 64), OP.add, l=QL)
+        quant(V("Fq%d" % t), V("Fs%d" % t), V("F"))
+        send(t)
+        ts(NL, V("tNP", 15, 128, 16), -2.0, V("sm", 8, 9), OP.mult, OP.add)
+        act(V("vL"), V("pcw"), AF.Copy, bias=-65.0, l=NL)
+        less(V("WD", 0, 384, 3), V("pcw", 17, 272, 2), V("vL"))
+        for p in range(2):
+            less(V("r", 16 + p, 272, 2), V("WD", 0, 384, 3), V("thB", p, 256, 2))
+        act(V("BB2"), V("r", 16, 272), AF.Copy, bias=-1e27, scale=2e27)
+        act(V("Sg"), V("r", 16, 272), AF.Sign, bias=0.5, scale=-1.0)
+        act(V("pen"), V("Sg"), AF.Copy, bias=192.0, scale=64.0)
+        ts(V("WM", 2, 384, 3), P, V("sm", 12, 13), None, OP.is_lt)
+        scan(V("WO"), V("WM"), V("WD"), 0.0, OP.mult, OP.add)
+        for p in range(2):
+            less(V("uu", p, 256, 2), V("pcw", 16 + p, 272, 2), V("WO", 2, 384, 3))
+        less(V("bv"), V("uu"), V("pen"))
+        scan(V("lm", 255, -1, -1), V("Sw", 263, 7, -1), V("BB2", 255, -1, -1), -1e25, OP.min, OP.max)
+        for h in range(2):
+            o, e = 128 * h + 1, 128 - h
+            tt(V("nE", o, o + e), V("ps%d" % h, 0, e), V("lm", o, o + e), OP.is_ge)
+        scan(V("D"), V("nE"), V("r", 15, 271), 0.0, OP.min, OP.max)
+        scan(V("D2", 255, -1, -1), V("nW", 255, -1, -1), V("D", 255, -1, -1), 1.0, OP.max, OP.min)
+        scan(V("vl"), V("D2"), V("bv"), 0.0, OP.mult, OP.max)
+        ts(V("u2"), V("vl"), 0.0, None, OP.is_equal)
+        scan(V("hv", 255, -1, -1), V("u2", 255, -1, -1), V("vl", 255, -1, -1), 0.0, OP.mult, OP.add)
+        dscan(V("tsb"), V("hv"), V("dL2"))
+        ts(HL, V("tsb", 15, 256, 16), V("sm", 9, 10), None, OP.add)
+        if t == R - 1:
+            act(V("s64"), V("col"), AF.Copy, l=EL)
+            act(V("out"), V("s64"), AF.Copy, l=HL)
+            dma("s", T.ol[:, :], T.out[0:128:16, :], [V("out")], [])
+        X = "X%d" % ((t + 1) % 2)
+        for b in (0, 3, 1, 2):
+            o = ("pst", "ps1", "ps0", "psr")[b]
+            mm(V(o, 0, 128), V("wq", 128 * b, 128 * b + 128), V("wp", 128 * b, 128 * b + 128), V("lc%d" % t), V("ls%d" % t))
+            if b == 0:
+                ts(V("H", 0, 64), V(o, 0, 64), 0.0, 0.03125, OP.max, OP.mult)
+            else:
+                act(V("H", 64 * b, 64 * b + 64), V(o, 0, 64), AF.Relu, scale=0.03125)
+        for h in range(2):
+            hl = V("su", 24 + 8 * h, 32 + 8 * h)
+            for b in (0, 1, 3, 2) if h == 0 else (0, 3, 2, 1):
+                o = 256 * b + 128 * h
+                x = V(X, 512 * h + b, 512 * h + 512, 4)
+                if b < 2 - h:
+                    tt(x, V("H", 64 * b, 64 * b + 64), V("Tf", o, o + 128), OP.add, l=hl)
+                else:
+                    k = 512 if b == 1 else o - 512
+                    act(V("G3", k, k + 128), V("H", 64 * b, 64 * b + 64), AF.Copy, l=hl)
+                    tt(x, V("pst", 512 * b + 128 * h, 512 * b + 128 * h + 128), V("G3", k, k + 128), OP.add)
+    product("vq", "vs", "X%d" % (R % 2), ("ps",))
+    dma("a", T.oc[:, :], T.XQ[:, :].bitcast(dt.uint8), [XQ], [])
+    for k in range(4):
+        dma("a" if k % 2 else "s", T.osc[4 * k:4 * k + 4, :], T.XS[32 * k:32 * k + 4, :], [XS], [])
+    copy(V("yb", 0, 128), V("ps0", 0, 128))
+    copy(V("yb", 128, 256), V("ps1", 0, 128))
+    dma("s", T.y[:, :], T.yb[:, :], [V("yb")], [])
+    issue()

@@ -6,42 +6,39 @@ import comms_topo
 C, K, R = 256, 64, 3
 STEP = [1, 2, 4]
 F32, B16, I32, U16, U8, MX = "float32", "bfloat16", "int32", "uint16", "uint8", "float8_e4m3fn_x4"
-INIT = float(2 ** 20 + 256)
-LIFT, LIFT2 = float(2 ** 21), 128.0
-BASE = 192.0
-ALL = 66560
-SPAN = C - K + 16
+EPS = 2.0 ** -19
+LIFT = float(2 ** 21)
+U = 128.0
+BASE = 64.0 * U
 CYCLE, FIXED, WAKE, NET = 0.83, 0.0, 220.0, 2500.0
 CASES = ((1.0, 190.0, 3500.0), (1.0, 240.0, 2500.0), (1.25, 210.0, 2500.0))
 TRIES = 7000
 ORDERS = {}
 
 _SB = {
-    F32: {"sm": 64, "c8": 8, "Sw": 784, "M": 128, "VV": 128, "PK": 128, "tmV": 256,
-          "tmM": 128, "tmN": 128, "tsV": 256, "tsM": 128, "tsN": 128, "tRL": 128, "tRR": 128, "tNP": 128, "NJ": 128, "nkL": 136,
-          "Gp": 128, "np": 128, "CT": 256, "g128": 128, "s128": 128, "s64": 64, "H": 256, "G3": 640, "lm": 256, "out": 256,
-          "yb": 256},
+    F32: {"sm": 64, "c8": 8, "Sw": 528, "M": 128, "VV": 128, "PK": 128, "tmV": 256,
+          "tmM": 128, "tmN": 128, "tsV": 256, "tsM": 128, "tsN": 128, "tR": 256, "tNP": 128, "NJ": 128, "nkL": 136, "RP0": 384, "RP1": 384,
+          "np": 128, "s64": 64, "H": 256, "G3": 640, "out": 256, "yb": 256, "ka": 128, "kc": 128, "fw": 64},
     B16: {"X0": 1024, "X1": 1024, "ut": 512, "vt": 512, "et": 520, "et1": 520, "rbt": 512, "zt": 512, "one": 64, "idn": 128, "A": 272, "A2": 272,
-          "du": 256, "pk": 256, "npk": 256, "np2": 256, "ni": 256, "nf": 256, "th": 256, "thB": 256, "hpx": 256, "hp": 128, "FV": 1024, "FE": 512,
-          "UL": 1040, "UR": 1040, "K": 256, "pcw": 272, "ed": 416, "ec": 416, "cn": 416, "Tf": 512, "Th": 2048, "TE": 256, "F": 512,
-          "tsb": 256, "vL": 128, "nW": 256, "vl": 256, "hv": 256, "WM": 384, "WD": 384, "WO": 384, "r": 272},
-    U16: {"su": 64},
+          "du": 256, "hpx": 256, "hp": 128, "FV": 1024, "FE": 512, "UL": 1040, "UR": 1040, "ed": 416, "F": 512, "TU": 2048, "BI": 1024,
+          "Ct": 144, "HT": 192, "colT": 320, "hc": 256, "NP0": 128, "NP1": 128},
+    U16: {"su": 96},
     MX: {"uq0": 128, "uq": 128, "vq": 128, "wq": 512, "eq": 512, "rbq": 128, "zq": 128, "FVq": 256, "FEq": 128, "XQ": 256},
     U8: {"us0": 128, "us": 128, "vs": 128, "wp": 512, "es": 512, "rbs": 128, "zs": 128, "FVs": 256, "FEs": 128, "XS": 256},
 }
-for _n, _d in (("RL", F32), ("RR", F32), ("NP", B16)):
-    for _h in "01":
-        _SB[_d][_n + _h] = 128
 for _t in range(R):
     for _n, _d in (("Fq", MX), ("Fs", U8), ("lc", MX), ("ls", U8)):
         _SB[_d]["%s%d" % (_n, _t)] = 128
 _JOINT = {
-    "kf": (F32, {"iw": 776, "cf": 256, "jc": 128, "col": 256, "cq": 8}),
-    "kb": (B16, {"mk": 256, "sgb": 128, "par": 256, "mkS": 64, "dg": 776, "ng": 144, "mP": 128, "rst": 128, "mkV": 256, "rstV": 256, "dL": 128,
-                 "dL2": 256, "mt": 256, "mu": 256}),
+    "kf": (F32, {"cf": 256, "jc": 128, "cq": 8, "cw": 8, "b0": 4}),
+    "kb": (B16, {"mk": 256, "par": 256, "ng": 144, "mP": 128, "rst": 128, "mkV": 256, "rstV": 256, "dL": 64, "dL2": 128, "dL3": 256, "dX": 128,
+                 "mt": 256, "mu": 256, "pv": 256, "fv": 64}),
     "ki": (I32, {"ci": 256, "cj": 256, "c0": 8, "c1": 8, "c2": 8}),
-    "rb": (B16, {"uu": 256, "u2": 256, "bv": 256, "BB2": 256, "nE": 256, "Sg": 256, "pen": 256, "D": 256, "D2": 256}),
-    "l8s": (I32, {"k8": 8, "l8": 8}),
+    "eb": (B16, {"As": 128, "dA": 128, "npk": 256, "ni": 256, "mB": 258, "ph": 128, "fl": 64, "pf": 64, "fx": 64, "sv": 256, "nW": 256, "nW2": 256,
+                 "d0": 256, "F1": 256, "u1": 256, "h1": 256, "t1": 256}),
+    "rb": (B16, {"K": 128, "pK": 128, "Cm": 128, "Kc": 128, "y": 129, "bw": 128, "pen": 128, "bv": 128, "gl": 128, "vl": 128, "u2": 128,
+                 "tsb": 256}),
+    "l8s": (I32, {"k8": 8, "l8": 8, "q8": 8, "s8": 8}),
 }
 WIDTH = {n: w for l in _SB.values() for n, w in l.items()}
 TYPE = {n: d for d, l in _SB.items() for n in l}
@@ -277,10 +274,10 @@ def rank_program(g, core, T, topo):
             do("v", lambda e: e.tensor_scalar(ap(out), ap(a), sc(s1), sc(s2), op0, op1), [a] + scr(s1, s2), [out], half(out, a))
 
     def scan(out, d0, d1, init, op0, op1):
-        do("v", lambda e: e.tensor_tensor_scan(ap(out), ap(d0), ap(d1), init, op0, op1), [d0, d1], [out], half(out, d0, d1))
+        do("v", lambda e: e.tensor_tensor_scan(ap(out), ap(d0), ap(d1), sc(init), op0, op1), [d0, d1] + scr(init), [out], half(out, d0, d1))
 
-    def copy(out, a):
-        do("v", lambda e: e.tensor_copy(ap(out), ap(a)), [a], [out], half(out, a))
+    def copy(out, a, l=None):
+        do("v", lambda e: e.tensor_copy(ap(out), ind(a, l) if l else ap(a)), [a] + scr(l), [out], 60 + 1.5 * width(out) if l else half(out, a))
 
     def fill(v, c):
         do("v", lambda e: e.memset(ap(v), c), [], [v], half(v))
@@ -323,13 +320,14 @@ def rank_program(g, core, T, topo):
     def less(out, a, b):
         scan(out, a, b, 0.0, OP.max, OP.subtract)
 
-    LI, EL, QL, NL, HL, UO = V("su", 0, 8), V("su", 8, 12), V("su", 12, 16), V("su", 16, 24), V("su", 24, 40), V("su", 40, 48)
+    LI, EL, NL, HL, UO = V("su", 0, 8), V("su", 8, 12), V("su", 16, 24), V("su", 24, 40), V("su", 40, 48)
+    PL, LQ, N3, CL = V("su", 48, 56), V("su", 56, 64), V("su", 64, 72), V("su", 72, 88)
 
     dma("s", ap(V("X0")), T.x[:, :], [], [V("X0")])
     dma("a", ap(V("ut")), T.u[:, :], [], [V("ut")])
-    dma("s", ap(V("wq")).bitcast(dt.uint8), T.wc[:, :], [], [V("wq")])
-    dma("a", ap(V("wp")), T.ws[:, :], [], [V("wp")])
-    dma("s", ap(V("vt")), T.v[:, :], [], [V("vt")])
+    dma("s", ap(V("wq")).bitcast(dt.uint8), T.wc[:, :], [V("X0"), V("ut")], [V("wq")])
+    dma("s", ap(V("wp")), T.ws[:, :], [V("X0"), V("ut")], [V("wp")])
+    dma("s", ap(V("vt")), T.v[:, :], [V("X0"), V("ut")], [V("vt")])
 
     iota(V("ci"), [[1, 256]], 256, -1)
     bits(V("cj"), V("ci"), 15)
@@ -337,32 +335,27 @@ def rank_program(g, core, T, topo):
     ts(V("mk"), V("cf"), 0.0, None, OP.is_equal)
     iota(V("c0"), [[16, 8]], 0, 0)
     copy(UO, V("c0"))
-    for n, w, k, c0, c in (("sgb", 128, 32, 0.0, 1.0), ("par", 256, 2, 0.0, 1.0), ("rst", 128, 16, -4.95e29, 4.95e29), ("rstV", 256, 32, 4.95e29, -4.95e29)):
+    for n, w, k, c0, c in (("par", 256, 2, 0.0, 1.0), ("rst", 128, 16, -4.95e29, 4.95e29), ("rstV", 256, 32, 4.95e29, -4.95e29)):
         fill(V(n, 0, w), c)
         fill(V(n, 0, w, k), c0)
-    for a, b in ((0, 8), (264, 520), (776, 784)):
-        fill(V("Sw", a, b), -1e25)
+    fill(V("Sw", 0, 8), -1e25)
+    fill(V("Sw", 264, 528), -1e25)
     for p in range(2):
         ts(V("mkV", p, 256, 2), V("mk", 0, 128), 0.5, -9.9e29, OP.subtract, OP.mult)
     ts(V("tmV", 0, 1), V("mkV", 0, 1), -1e25, None, OP.max)
     ts(V("mP"), V("mk", 0, 128), 0.5, 9.9e29, OP.subtract, OP.mult)
-    for d, n, c in (("dL", 128, LIFT), ("dL2", 256, LIFT2)):
+    for d, n, w, c0, c in (("dL", 64, 1, -1e29, LIFT), ("dX", 64, 2, 1e29, -LIFT * EPS), ("dL2", 128, 1, -1e29, 128.0 * U), ("dL3", 256, 1, 1e29, -192.0)):
         ts(V("mt", 0, n), V("mk", 0, n), c, None, OP.mult)
-        ts(V("mu", 0, n), V("mk", 0, n), -1e29, None, OP.mult)
+        ts(V("mu", 0, n), V("mk", 0, n), c0, None, OP.mult)
         copy(V(d, 0, 1), V("mu", 0, 1))
-        tt(V(d, 1, n), V("mu", 1, n), V("mt", 0, n - 1), OP.add)
-    ts(V("mkS"), V("mk", 0, 64), -2.0 ** 20, 2.0 ** 20, OP.mult, OP.add)
-    fill(V("dg"), -65.0)
-    fill(V("dg", 512, 768), -1.0)
-    for k, c in enumerate((0.0, 1.0)):
-        fill(V("WM", k, 384, 3), c)
-    fill(V("WD", 2, 384, 3), 64.0)
+        tt(V(d, w, n * w, w), V("mu", 1, n), V("mt", 0, n - 1), OP.add)
+    ts(V("dX", 1, 128, 2), V("mk", 0, 64), 512.0 * EPS, None, OP.mult)
     quant(V("uq0"), V("us0"), V("ut"))
     do("v", lambda e: e.tensor_copy(T.uq[:, 0:128].bitcast(dt.uint32), T.uq0[:, 0:128].bitcast(dt.uint32).indirect(ap(UO))), [V("uq0"), UO], [V("uq")], 250)
     act(V("us"), V("us0", 0, 128), AF.Copy, l=UO)
     fill(V("idn"), 1.0)
     fill(V("one"), 1.0)
-    fill(V("c8"), 1024.0)
+    fill(V("c8"), 1024.0 * EPS)
     select(V("c8"), [[-16, 8]], OP.is_ge, 0, 1)
     select(V("c8"), [[16, 8]], OP.is_ge, 15, -1)
     for m in range(8):
@@ -370,12 +363,15 @@ def rank_program(g, core, T, topo):
     select(V("idn"), [[-1, 128]], OP.is_equal, 0, 1)
     iota(V("c1"), [[0, 8]], 0, 1)
     iota(V("jc"), [[2, 128]], 131072, 0)
+    act(V("jc"), V("jc"), AF.Copy, scale=EPS)
     iota(V("ng", 16, 144), [[-1, 128]], 128, 0)
-    iota(V("iw", 0, 256), [[1, 256]], ALL + 256, 0)
-    level("iw", 256, 512, ALL)
-    iota(V("iw", 512, 768), [[1, 256]], ALL + 256, 0)
-    level("iw", 768, 776, ALL)
-    iota(V("col"), [[1, 256]], 0, 0)
+    iota(V("pv"), [[1, 128], [0, 2]], 1, 0)
+    iota(V("fv"), [[1, 64]], 129, 0)
+    iota(V("b0"), [[24, 4]], 81, 0)
+    iota(V("cw"), [[32, 8]], 0, 0)
+    iota(V("HT", 128, 192), [[int(U), 64]], int(U), 0)
+    iota(V("colT", 0, 256), [[1, 256]], -1, 0)
+    iota(V("colT", 256, 320), [[1, 64]], 0, 0)
     for n, o in (("et", 4), ("et1", 5)):
         fill(V(n), 0.0)
         act(V(n, o, o + 509, 4), V("idn"), AF.Copy)
@@ -386,15 +382,16 @@ def rank_program(g, core, T, topo):
     bits(V("c2"), V("c1"), 15)
     copy(V("cq"), V("c2"))
     for m in range(4):
-        ts(V("sm", m, m + 1), V("cq", 0, 1), 16.0 * m + BASE + 0.5, None, OP.add)
+        ts(V("sm", m, m + 1), V("cq", 0, 1), U, (16.0 * m + 0.5) * U + BASE, OP.mult, OP.add)
     ts(V("sm", 11, 12), V("cq", 0, 1), 15.0, None, OP.is_lt)
-    ts(V("sm", 8, 9), V("sm", 11, 12), 2.0 * LIFT, 273.0, OP.mult, OP.add)
-    ts(V("sm", 9, 10), V("sm", 11, 12), -LIFT2, -1.0, OP.mult, OP.add)
-    for v, c in ((V("A"), 0.0), (V("nW"), 1.0), (V("UL", 15, 16), 1.0), (V("UR", 1024, 1025), 1.0), (V("nkL", 128, 129), 0.0), (V("ng", 15, 16), 0.0),
-                 (V("pcw", 0, 16), BASE), (V("nE"), 1.0), (V("r", 0, 16), 0.0)):
+    for k, c, c0 in ((8, LIFT, 129.0), (9, -128.0, -1.0), (13, 192.0, -1.0), (14, -LIFT, 127.0), (15, 96.0, 0.0)):
+        ts(V("sm", k, k + 1), V("sm", 11, 12), c, c0, OP.mult, OP.add)
+    ts(V("sm", 15, 16), V("cq", 0, 1), V("sm", 15, 16), 2.0, OP.add, OP.mult)
+    ts(V("cw"), V("cw"), V("sm", 15, 16), None, OP.add)
+    for v, c in ((V("A", 256, 257), 0.0), (V("nW", 0, 1), 1.0), (V("UL", 15, 16), 1.0), (V("UR", 1024, 1025), 1.0), (V("nkL", 128, 129), 0.0),
+                 (V("ng", 15, 16), 0.0), (V("Ct", 0, 1), BASE), (V("mB", 0, 2), 2.0 * U), (V("y", 0, 1), U)):
         fill(v, c)
     level("FE", 0, 512, 0)
-    level("g128", 0, 128, 0)
     level("F", 256, 512, 0)
     level("zt", 0, 512, 0)
     quant(V("zq"), V("zs"), V("zt"))
@@ -420,7 +417,7 @@ def rank_program(g, core, T, topo):
         add("in", None, [V("Fq%d" % t)], [V("lc%d" % t, 0, 64), V("ls%d" % t, 0, 64)], NET, 0.0, "arr%d" % t, 2 * len(engs))
 
     XQ, XS, P = V("XQ"), V("XS"), V("psr", 0, 128)
-    pc = V("pcw", 16, 272)
+    Cn = V("Ct", 1, 129)
 
     def product(l, ls, X, banks):
         for h in range(2):
@@ -441,13 +438,8 @@ def rank_program(g, core, T, topo):
         o = 512 * (m // 4) + m % 4
         return V("FV", o + 4 * a, 512 * (m // 4) + 4 * b, 4)
 
-    def climb(n, d, o, init, w):
-        for m in range(7, -1, -1):
-            k = 16 * m + 15 + (m == 0)
-            scan(V("%s%d" % (n, m // 4), 80 + 16 * (m % 4) - k, 80 + 16 * (m % 4)), V("UL", 144 * m + 31 - k, 144 * m + 31),
-                 V(d, o + 16 * m + 15 - k, o + 16 * m + 15), init, OP.mult, OP.max)
-        for h in range(2):
-            dscan(V(w, 64 * h, 64 * h + 64), V("%s%d" % (n, h), 64, 128), V("dL", 0, 64))
+    def Tf(b, a=0, e=256):
+        return V("TU", 512 * b + 256 + a, 512 * b + 256 + e)
 
     for t in range(R):
         product("uq", "us", "X%d" % (t % 2), ("ps", "pst"))
@@ -473,8 +465,12 @@ def rank_program(g, core, T, topo):
                 act(slot(m), V("VV"), AF.Sign, bias=s, scale=-1.0)
         scan(V("tmM"), V("M"), V("mP"), -4e29, OP.max, OP.min)
         scan(V("tsM"), V("rst"), V("tmM"), 0.0, OP.min, OP.max)
-        dma("s", T.Sw[:, 520:776], T.Sw[:, 8:264], [V("Sw", 8, 264)], [V("Sw", 520, 776)])
-        scan(V("NJ"), V("A", 0, 256, 2), V("jc"), 0.0, OP.max, OP.subtract)
+        ts(V("As"), V("A", 0, 256, 2), EPS, None, OP.mult)
+        less(V("NJ"), V("As"), V("jc"))
+        scan(V("dA"), V("dL3", 0, 128), V("A", 1, 256, 2), 0.0, OP.add, OP.min)
+        tt(V("sm", 40, 48), V("dA", 15, 128, 16), V("cw"), OP.add)
+        copy(PL, V("sm", 40, 48))
+        ts(V("sm", 48, 56), V("sm", 40, 48), EPS, 2.0 + 256.0 * EPS, OP.mult, OP.add)
         for m in range(8):
             s = V("tsM", 16 * m + 15, 16 * m + 16)
             act(V("UL", 16 + 128 * m, 16 + 128 * m + 16 * m + 16), V("M", 0, 16 * m + 16), AF.Sign, bias=s, scale=-1.0)
@@ -486,30 +482,33 @@ def rank_program(g, core, T, topo):
                 act(r, r, AF.Sign, bias=0.5)
         ranks((0, 1))
         tt(V("nkL", 0, 128), P, V("NJ"), OP.subtract)
-        act(V("A2", 0, 257), V("A", 0, 257), AF.Copy, bias=2.0)
+        act(V("A2", 0, 257), V("A", 0, 257), AF.Copy, bias=512.0, scale=256.0)
         less(V("du"), V("A2", 0, 256), V("A2", 1, 257))
         scan(V("hpx"), V("par"), V("du"), 0.0, OP.mult, OP.max)
-        ts(V("hp"), V("hpx", 1, 256, 2), 2e29, -1e27, OP.mult, OP.add)
+        ts(V("hp"), V("hpx", 1, 256, 2), 8e26, -1e27, OP.mult, OP.add)
         scan(V("PK"), V("hp"), V("M"), 0.0, OP.add, OP.min)
-        act(V("pk"), V("du"), AF.Relu)
-        act(V("npk"), V("pk"), AF.Copy, bias=1.0, scale=-1.0)
-        act(V("np2"), V("pk"), AF.Copy, bias=132096.0, scale=-65536.0)
         for b in range(4):
-            act(V("Th", 512 * b, 512 * b + 256), V("pst", 512 * b, 512 * b + 256), AF.Copy, scale=0.5)
-            dma("s", T.Th[:, 512 * b + 256:512 * b + 512], T.Th[:, 512 * b:512 * b + 256], [V("Th", 512 * b, 512 * b + 256)],
-                [V("Th", 512 * b + 256, 512 * b + 512)])
-        climb("RL", "nkL", 1, INIT, "tRL")
+            act(Tf(b), V("pst", 512 * b, 512 * b + 256), AF.Copy)
+            act(V("BI", 256 * b, 256 * b + 256, 2), Tf(b), AF.Copy, scale=0.5, l=PL)
+        for m in range(7, -1, -1):
+            k, o = 16 * m + 15 + (m == 0), 80 + 16 * (m % 4)
+            scan(V("RP%d" % (m // 4), 2 * (o - k) + 1, 2 * o, 2), V("UL", 144 * m + 31 - k, 144 * m + 31), V("nkL", 16 * m + 16 - k, 16 * m + 16),
+                 V("sm", 48 + m, 49 + m), OP.mult, OP.max)
         for m in range(8):
-            a, e = 16 * m, 127 + m // 7
-            scan(V("RR%d" % (m // 4), e - 1 - a + a % 64, a % 64 - 1, -1), V("UR", 128 * m + e, 128 * m + a, -1), V("nkL", e, a, -1), INIT, OP.mult,
-                 OP.max)
+            a, e, o = 16 * m, 127 + m // 7, 64 + 16 * (m % 4)
+            scan(V("RP%d" % (m // 4), 2 * (o + e - 1 - a), 2 * o - 1, -2), V("UR", 128 * m + e, 128 * m + a, -1), V("nkL", e, a, -1),
+                 V("sm", 48 + m, 49 + m), OP.mult, OP.max)
         for h in range(2):
-            dscan(V("tRR", 64 * h, 64 * h + 64), V("RR%d" % h, 0, 64), V("dL", 0, 64))
-        ts(V("sm", 40, 48), V("tRR", 15, 128, 16), 512.0, None, OP.add)
-        tt(V("k8"), V("tRL", 15, 128, 16), V("sm", 40, 48), OP.min)
-        bits(V("l8"), V("k8"), 1023)
+            scan(V("tR", 128 * h, 128 * h + 128), V("dX"), V("RP%d" % h, 128, 256), 0.0, OP.add, OP.min)
+        ts(V("k8"), V("tR", 31, 256, 32), 1.0 / EPS, LIFT, OP.mult, OP.add)
+        bits(V("l8"), V("k8"), 511)
         copy(LI, V("l8"))
-        tt(V("np"), V("Sw", 8, 784), V("PK"), OP.subtract, l=LI)
+        tt(V("np"), V("Sw", 8, 520), V("PK"), OP.subtract, l=LI)
+        bits(V("q8"), V("k8"), 255)
+        copy(LQ, V("q8"))
+        for b in range(4):
+            act(V("BI", 256 * b + 1, 256 * b + 256, 2), Tf(b), AF.Copy, scale=0.5, l=LQ)
+            scan(V("TU", 512 * b, 512 * b + 256), V("par"), V("BI", 256 * b, 256 * b + 256), 0.0, OP.mult, OP.add)
         scan(V("tmN"), V("np"), V("mP"), -4e29, OP.max, OP.min)
         scan(V("tsN", 127, -1, -1), V("rst"), V("tmN", 127, -1, -1), 0.0, OP.min, OP.max)
         for m in range(8):
@@ -523,67 +522,75 @@ def rank_program(g, core, T, topo):
                 ts(slot(m, 0, 16 * m), V("np", 0, 16 * m), s, None, OP.is_le)
         tt(V("FE", 0, 512, 4), V("np"), V("tsN"), OP.is_equal)
         ranks((2, 1, 0))
-        act(V("Gp"), V("iw"), AF.Copy, l=LI)
-        act(V("WD", 1, 384, 3), V("dg"), AF.Copy, l=LI)
+        ts(V("npk"), V("du"), 0.5, U, OP.is_lt, OP.mult)
         scan(V("ni"), V("npk"), V("npk"), 0.0, OP.add, OP.max)
-        ts(V("sm", 10, 11), V("ni", 255, 256), -float(2 ** 20), 192.0 * 2 ** 20, OP.mult, OP.add)
-        ts(V("sm", 12, 13), V("sm", 10, 11), float(ALL), float(ALL), OP.add, OP.min)
-        act(V("nf"), V("ni"), AF.Relu, bias=V("sm", 10, 11), scale=float(2 ** 20))
-        scan(V("th"), V("nf"), V("np2"), 0.0, OP.max, OP.min)
-        ts(V("thB"), V("th"), float(ALL), 2.0 ** -10, OP.max, OP.mult)
-        climb("NP", "ng", 16, 200.0, "tNP")
-        for p in range(2):
-            tt(V("K", p, 256, 2), P, V("th", p, 256, 2), OP.is_ge)
-        scan(pc, V("K"), V("K"), BASE, OP.add, OP.max)
+        ts(V("sm", 10, 11), V("ni", 255, 256), -192.0 * U, 0.0, OP.add, OP.max)
+        ts(V("sm", 12, 13), V("sm", 10, 11), 1024.0 * EPS / U, 65.0 * 1024.0 * EPS, OP.mult, OP.add)
+        ts(V("mB", 2, 258), V("ni"), V("sm", 10, 11), 2.0 * U, OP.min, OP.add)
+        less(V("ph"), V("mB", 2, 258, 2), V("mB", 0, 256, 2))
+        less(V("fl"), V("mB", 2, 66), V("mB", 1, 65))
+        ts(V("pf"), V("fl"), -2.0, 256.0, OP.mult, OP.add)
+        less(V("fx"), V("fv"), V("pf"))
+        dscan(V("fw"), V("fx"), V("dL"))
+        ts(V("sm", 20, 24), V("fw", 15, 64, 16), V("sm", 14, 15), None, OP.add)
+        ts(V("sm", 24, 28), V("sm", 20, 24), 128.0, None, OP.is_lt)
+        tt(V("sm", 28, 32), V("sm", 20, 24), V("b0"), OP.max)
+        for m in range(7, -1, -1):
+            k, o = 16 * m + 15 + (m == 0), 80 + 16 * (m % 4)
+            scan(V("NP%d" % (m // 4), o - k, o), V("UL", 144 * m + 31 - k, 144 * m + 31), V("ng", 16 * m + 31 - k, 16 * m + 31), 200.0, OP.mult,
+                 OP.max)
+        for h in range(2):
+            dscan(V("tNP", 64 * h, 64 * h + 64), V("NP%d" % h, 64, 128), V("dL"))
+        ts(V("sm", 32, 40), V("tNP", 15, 128, 16), -1.0, V("sm", 8, 9), OP.mult, OP.add)
+        copy(NL, V("sm", 32, 40))
+        bits(V("s8"), V("k8"), 768)
+        tt(V("sm", 56, 64), V("sm", 32, 40), V("s8"), OP.subtract)
+        copy(N3, V("sm", 56, 64))
+        less(V("sv"), V("pv"), V("npk"))
+        tt(V("sv", 0, 64), V("sv", 0, 64), V("fx"), OP.max)
+        act(V("nW2"), V("nW"), AF.Copy, bias=512.0, scale=256.0)
+        less(V("d0"), V("nW2"), V("A2", 0, 256))
+        scan(V("F1"), V("d0"), V("sv"), 0.0, OP.min, OP.max)
+        ts(V("u1"), V("F1"), 0.0, None, OP.is_le)
+        scan(V("h1", 255, -1, -1), V("u1", 255, -1, -1), V("F1", 255, -1, -1), 0.0, OP.mult, OP.max)
+        scan(V("t1"), V("dL3"), V("h1"), 0.0, OP.add, OP.min)
+        ts(CL, V("t1", 15, 256, 16), V("sm", 13, 14), None, OP.add)
+        ts(V("K"), P, V("sm", 12, 13), U, OP.is_ge, OP.mult)
+        scan(Cn, V("K"), V("ph"), BASE, OP.add, OP.add)
         for m in range(4):
-            w, o = V("pcw", 16 + 16 * m, 16 + 16 * m + SPAN), SPAN * (m % 2)
-            if m < 2:
-                ts(V("ec", o, o + SPAN), w, V("sm", m, m + 1), None, OP.is_le)
-                scan(V("cn", o, o + SPAN), V("ec", o, o + SPAN), V("ec", o, o + SPAN), 16.0 * m, OP.add, OP.max)
+            act(V("ed", 104 * m, 104 * m + 80 + 8 * m), V("Ct", 1 + 8 * m, 81 + 16 * m), AF.Sign, bias=V("sm", m, m + 1), scale=-1.0,
+                acc=V("sm", 16 + m, 17 + m))
+            ts(V("su", 8 + m, 9 + m), V("sm", 16 + m, 17 + m), V("sm", 24 + m, 25 + m), V("sm", 28 + m, 29 + m), OP.mult, OP.add)
+        for b in range(4):
+            if b % 2:
+                act(V("F", b, 256, 4), V("TU", 512 * b, 512 * b + 320), AF.Copy, l=EL)
             else:
-                act(V("ed", o, o + SPAN), w, AF.Sign, bias=V("sm", m, m + 1), scale=-1.0, acc=V("sm", 16 + m, 17 + m))
-                ts(V("su", 8 + m, 9 + m), V("sm", 16 + m, 17 + m), 0.5, SPAN / 2.0 + 16.0 * m, OP.mult, OP.add)
-        copy(V("su", 8, 10), V("cn", SPAN - 1, 2 * SPAN, SPAN))
-        for b in range(2):
-            act(V("Tf", 256 * b, 256 * b + 256), V("pst", 512 * b, 512 * b + 256), AF.Copy)
-        for b in range(4):
-            act(V("TE", 64 * b, 64 * b + 64), V("Th", 512 * b, 512 * b + 256), AF.Copy, l=EL)
-        for p in range(2):
-            less(V("CT", p, 256, 2), V("np2", p, 256, 2), V("Gp"))
-        ts(V("g128", 31, 128, 32), EL, -1.0, None, OP.mult)
-        tt(V("g128", 0, 128, 2), V("CT"), V("mkS"), OP.add, l=EL)
-        scan(V("s128"), V("sgb"), V("g128"), 0.0, OP.mult, OP.min)
-        ts(QL, V("s128", 31, 128, 32), -1.0, None, OP.mult)
-        for b in range(4):
-            tt(V("F", b, 256, 4), V("Th", 512 * b, 512 * b + 512), V("TE", 64 * b, 64 * b + 64), OP.add, l=QL)
+                copy(V("F", b, 256, 4), V("TU", 512 * b, 512 * b + 320), l=EL)
         quant(V("Fq%d" % t), V("Fs%d" % t), V("F"))
         send(t)
-        ts(NL, V("tNP", 15, 128, 16), -2.0, V("sm", 8, 9), OP.mult, OP.add)
-        act(V("vL"), V("pcw"), AF.Copy, bias=-65.0, l=NL)
-        less(V("WD", 0, 384, 3), V("pcw", 17, 272, 2), V("vL"))
-        for p in range(2):
-            less(V("r", 16 + p, 272, 2), V("WD", 0, 384, 3), V("thB", p, 256, 2))
-        act(V("BB2"), V("r", 16, 272), AF.Copy, bias=-1e27, scale=2e27)
-        act(V("Sg"), V("r", 16, 272), AF.Sign, bias=0.5, scale=-1.0)
-        act(V("pen"), V("Sg"), AF.Copy, bias=192.0, scale=64.0)
-        ts(V("WM", 2, 384, 3), P, V("sm", 12, 13), None, OP.is_lt)
-        scan(V("WO"), V("WM"), V("WD"), 0.0, OP.mult, OP.add)
-        for p in range(2):
-            less(V("uu", p, 256, 2), V("pcw", 16 + p, 272, 2), V("WO", 2, 384, 3))
-        less(V("bv"), V("uu"), V("pen"))
-        scan(V("lm", 255, -1, -1), V("Sw", 263, 7, -1), V("BB2", 255, -1, -1), -1e25, OP.min, OP.max)
-        for h in range(2):
-            o, e = 128 * h + 1, 128 - h
-            tt(V("nE", o, o + e), V("ps%d" % h, 0, e), V("lm", o, o + e), OP.is_ge)
-        scan(V("D"), V("nE"), V("r", 15, 271), 0.0, OP.min, OP.max)
-        scan(V("D2", 255, -1, -1), V("nW", 255, -1, -1), V("D", 255, -1, -1), 1.0, OP.max, OP.min)
-        scan(V("vl"), V("D2"), V("bv"), 0.0, OP.mult, OP.max)
+        scan(V("Cm"), V("K"), V("ph"), BASE - U, OP.add, OP.add)
+        tt(V("y", 1, 129), V("Ct", 0, 129), V("Cm"), OP.subtract, l=NL)
+        ts(V("pK"), V("K"), -128.0, 128.0 * U, OP.mult, OP.add)
+        less(V("Kc"), Cn, V("pK"))
+        tt(V("bw"), V("Ct", 0, 129), V("Kc"), OP.max, l=N3)
+        ts(V("pen"), V("y", 1, 129), 256.0, BASE, OP.mult, OP.max)
+        less(V("bv"), V("bw"), V("pen"))
+        scan(V("ka"), V("y", 0, 128), V("nkL", 0, 128), 0.0, OP.min, OP.max)
+        scan(V("kc", 127, -1, -1), V("nkL", 128, 0, -1), V("y", 128, 0, -1), 0.9, OP.max, OP.min)
+        tt(V("gl"), V("kc"), V("ka"), OP.is_gt)
+        scan(V("vl"), V("gl"), V("bv"), 0.0, OP.mult, OP.max)
         ts(V("u2"), V("vl"), 0.0, None, OP.is_equal)
-        scan(V("hv", 255, -1, -1), V("u2", 255, -1, -1), V("vl", 255, -1, -1), 0.0, OP.mult, OP.add)
-        dscan(V("tsb"), V("hv"), V("dL2"))
-        ts(HL, V("tsb", 15, 256, 16), V("sm", 9, 10), None, OP.add)
+        scan(V("HT", 127, -1, -1), V("u2", 127, -1, -1), V("vl", 127, -1, -1), 0.0, OP.mult, OP.add)
+        for h in range(2):
+            if h:
+                act(V("hc", 128, 256), V("HT"), AF.Copy, l=V("su", 80, 88))
+            else:
+                copy(V("hc", 0, 128), V("HT"), l=V("su", 72, 80))
+            dscan(V("tsb", 128 * h, 128 * h + 128), V("hc", 128 * h, 128 * h + 128), V("dL2", 0, 128))
+            ts(V("su", 24 + 8 * h, 32 + 8 * h), V("tsb", 128 * h + 15, 128 * h + 128, 16), 1.0 / U, V("sm", 9, 10), OP.mult, OP.add)
         if t == R - 1:
-            act(V("s64"), V("col"), AF.Copy, l=EL)
+            tt(V("colT", 1, 256, 2), V("colT", 1, 256, 2), V("A", 1, 256, 2), OP.add)
+            act(V("s64"), V("colT"), AF.Copy, l=EL)
             act(V("out"), V("s64"), AF.Copy, l=HL)
             dma("s", T.ol[:, :], T.out[0:128:16, :], [V("out")], [])
         X = "X%d" % ((t + 1) % 2)
@@ -600,7 +607,7 @@ def rank_program(g, core, T, topo):
                 o = 256 * b + 128 * h
                 x = V(X, 512 * h + b, 512 * h + 512, 4)
                 if b < 2 - h:
-                    tt(x, V("H", 64 * b, 64 * b + 64), V("Tf", o, o + 128), OP.add, l=hl)
+                    tt(x, V("H", 64 * b, 64 * b + 64), Tf(b, 128 * h, 128 * h + 128), OP.add, l=hl)
                 else:
                     k = 512 if b == 1 else o - 512
                     act(V("G3", k, k + 128), V("H", 64 * b, 64 * b + 64), AF.Copy, l=hl)

@@ -7,20 +7,21 @@ C, K, R = 256, 64, 3
 STEP = [1, 2, 4]
 F32, B16, I32, U16, U8, MX = "float32", "bfloat16", "int32", "uint16", "uint8", "float8_e4m3fn_x4"
 EPS = 2.0 ** -19
-LIFT = float(2 ** 21)
+LIFT, HUGE, ROUND = 2.0 ** 21, 2.0 ** 96, 1.5 * 2.0 ** 13
 U = 128.0
 BASE = 64.0 * U
 CYCLE, FIXED, WAKE, NET = 0.83, 0.0, 220.0, 2500.0
 CASES = ((1.0, 190.0, 3500.0), (1.0, 240.0, 2500.0), (1.25, 210.0, 2500.0))
-TRIES = 7000
+TRIES, ALIKE, SEED = 7000, 0.7, 0
+NV, NS = 2, 5
 ORDERS = {}
 
 _SB = {
     F32: {"sm": 64, "c8": 8, "Sw": 528, "M": 128, "VV": 128, "PK": 128, "tmV": 256,
-          "tmM": 128, "tmN": 128, "tsV": 256, "tsM": 128, "tsN": 128, "tR": 256, "tNP": 128, "NJ": 128, "nkL": 136, "RP0": 384, "RP1": 384,
+          "tmM": 128, "tmN": 128, "tsV": 256, "tsM": 128, "tsN": 128, "tR": 288, "d8": 8, "tNP": 128, "NJ": 128, "nkL": 136, "nkR": 136, "RP0": 464, "RP1": 400, "RP2": 336, "RP3": 272,
           "np": 128, "s64": 64, "H": 256, "G3": 640, "out": 256, "yb": 256, "ka": 128, "kc": 128, "fw": 64},
     B16: {"X0": 1024, "X1": 1024, "ut": 512, "vt": 512, "et": 520, "et1": 520, "rbt": 512, "zt": 512, "one": 64, "idn": 128, "A": 272, "A2": 272,
-          "du": 256, "hpx": 256, "hp": 128, "FV": 1024, "FE": 512, "UL": 1040, "UR": 1040, "ed": 416, "F": 512, "TU": 2048, "BI": 1024,
+          "du": 256, "hpx": 256, "hp": 128, "FV": 1024, "FE": 512, "UL": 1056, "ed": 416, "F": 512, "TU": 2048, "BI": 1024,
           "Ct": 144, "HT": 192, "colT": 320, "hc": 256, "NP0": 128, "NP1": 128},
     U16: {"su": 96},
     MX: {"uq0": 128, "uq": 128, "vq": 128, "wq": 512, "eq": 512, "rbq": 128, "zq": 128, "FVq": 256, "FEq": 128, "XQ": 256},
@@ -30,15 +31,15 @@ for _t in range(R):
     for _n, _d in (("Fq", MX), ("Fs", U8), ("lc", MX), ("ls", U8)):
         _SB[_d]["%s%d" % (_n, _t)] = 128
 _JOINT = {
-    "kf": (F32, {"cf": 256, "jc": 128, "cq": 8, "cw": 8, "b0": 4}),
-    "kb": (B16, {"mk": 256, "par": 256, "ng": 144, "mP": 128, "rst": 128, "mkV": 256, "rstV": 256, "dL": 64, "dL2": 128, "dL3": 256, "dX": 128,
-                 "mt": 256, "mu": 256, "pv": 256, "fv": 64}),
-    "ki": (I32, {"ci": 256, "cj": 256, "c0": 8, "c1": 8, "c2": 8}),
+    "kf": (F32, {"jc": 128, "cq": 8, "cw": 8, "b0": 4, "dX": 72}),
+    "kb": (B16, {"mk": 256, "par": 256, "ng": 144, "mP": 128, "rst": 128, "mkV": 256, "rstV": 256, "dL": 64, "dL2": 128, "dL3": 256,
+                 "mdL": 64, "mdL2": 128, "mdL3": 256, "edL": 64, "edL2": 128, "edL3": 256, "mt": 256, "pv": 256, "fv": 64}),
+    "ki": (I32, {"c0": 8, "c1": 8, "c2": 8}),
     "eb": (B16, {"As": 128, "dA": 128, "npk": 256, "ni": 256, "mB": 258, "ph": 128, "fl": 64, "pf": 64, "fx": 64, "sv": 256, "nW": 256, "nW2": 256,
                  "d0": 256, "F1": 256, "u1": 256, "h1": 256, "t1": 256}),
     "rb": (B16, {"K": 128, "pK": 128, "Cm": 128, "Kc": 128, "y": 129, "bw": 128, "pen": 128, "bv": 128, "gl": 128, "vl": 128, "u2": 128,
                  "tsb": 256}),
-    "l8s": (I32, {"k8": 8, "l8": 8, "q8": 8, "s8": 8}),
+    "l8s": (I32, {"k8": 8, "q8": 8, "s8": 8}),
 }
 WIDTH = {n: w for l in _SB.values() for n, w in l.items()}
 TYPE = {n: d for d, l in _SB.items() for n in l}
@@ -59,7 +60,7 @@ SEMAPHORES = ["qv", "qa", "qt", "qg"] + ["d%d" % i for i in range(48)] + ["arr%d
 
 def planner(g, T):
     eng = {"v": g.vector, "a": g.scalar, "t": g.tensor, "g": g, "s": g.sync}
-    ops, log = [], {}
+    ops, log, firsts, seen = [], {}, {}, {}
 
     def span(v):
         n, a, b, s = v
@@ -91,7 +92,10 @@ def planner(g, T):
                 if kind == "w" and x[3] == 1:
                     l[:] = [e for e in l if not (x[1] <= e[0][1] and e[0][2] <= x[2])]
                 l.append((x, kind, i))
-        ops.append({"q": q, "call": call, "pre": pre, "cost": cost, "hold": cost if hold is None else hold, "sem": sem or "q" + q, "inc": inc})
+        like = firsts.setdefault((q, str(writes or reads), seen.setdefault(str(writes or reads), [0])[0]), i)
+        seen[str(writes or reads)][0] += 1
+        ops.append({"q": q, "call": call, "pre": pre, "cost": cost, "hold": cost if hold is None else hold, "sem": sem or "q" + q, "inc": inc,
+                    "like": like})
 
     def best_order():
         n = len(ops)
@@ -166,14 +170,16 @@ def planner(g, T):
                 total += end
             return total
 
-        rng, at, best, least = np.random.default_rng(0), np.arange(n), None, 1e18
+        rng, best, least = np.random.default_rng(SEED), None, 1e18
+        alike = np.array([o["like"] for o in ops])
         for k in range(TRIES):
-            if k < 200:
-                noise, patience = rng.random(n) * (0.0, 100.0, 300.0, 800.0)[k // 4 % 4], (0.0, 20.0, 50.0, 100.0)[k % 4]
+            at = alike if k < TRIES * ALIKE else np.arange(n)
+            if k < 100:
+                noise, patience = (rng.random(n) * (0.0, 100.0, 300.0, 800.0)[k // 4 % 4])[at], (0.0, 20.0, 50.0, 100.0)[k % 4]
             else:
                 noise, patience = best[2].copy(), best[3] if k % 5 else 10.0 * (k // 5 % 11)
-                some = (np.abs(at - rng.integers(0, n)) < (5, 20, 60, 200)[k % 4]) & (rng.random(n) < (0.6, 0.3, 0.15, 0.1)[k % 4])
-                noise[some] += rng.normal(0.0, (100.0, 300.0, 800.0)[k % 3], int(some.sum()))
+                some = (np.abs(np.arange(n) - at[rng.integers(0, n)]) < (3, 10, 30, 100)[k % 4]) & (rng.random(n) < (0.6, 0.3, 0.15, 0.1)[k % 4])
+                noise += (some * rng.normal(0.0, (100.0, 300.0, 800.0)[k % 3], n))[at]
             end, out = order([r + x for r, x in zip(rank, noise.tolist())], patience)
             if end > least + 500.0:
                 continue
@@ -211,7 +217,7 @@ def planner(g, T):
         for s in sorted(count):
             if known["g"].get(s, 0) < count[s]:
                 g.wait_ge(T.sem[s], count[s])
-    return add, issue
+    return add, issue, seen
 
 
 def rank_program(g, core, T, topo):
@@ -219,7 +225,7 @@ def rank_program(g, core, T, topo):
     if rank is None:
         return
     OP, AF = AluOpType, ActivationFunctionType
-    add, issue = planner(g, T)
+    add, issue, seen = planner(g, T)
     nd = [0]
 
     def V(n, a=None, b=None, s=1):
@@ -329,10 +335,11 @@ def rank_program(g, core, T, topo):
     dma("s", ap(V("wp")), T.ws[:, :], [V("X0"), V("ut")], [V("wp")])
     dma("s", ap(V("vt")), T.v[:, :], [V("X0"), V("ut")], [V("vt")])
 
-    iota(V("ci"), [[1, 256]], 256, -1)
-    bits(V("cj"), V("ci"), 15)
-    copy(V("cf"), V("cj"))
-    ts(V("mk"), V("cf"), 0.0, None, OP.is_equal)
+    iota(V("c1"), [[0, 8]], 0, 1)
+    iota(V("mt"), [[0, 16], [1, 16]], 0, 0)
+    bits(V("c2"), V("c1"), 15)
+    copy(V("cq"), V("c2"))
+    ts(V("mk"), V("mt"), V("cq", 0, 1), None, OP.is_equal)
     iota(V("c0"), [[16, 8]], 0, 0)
     copy(UO, V("c0"))
     for n, w, k, c0, c in (("par", 256, 2, 0.0, 1.0), ("rst", 128, 16, -4.95e29, 4.95e29), ("rstV", 256, 32, 4.95e29, -4.95e29)):
@@ -344,12 +351,17 @@ def rank_program(g, core, T, topo):
         ts(V("mkV", p, 256, 2), V("mk", 0, 128), 0.5, -9.9e29, OP.subtract, OP.mult)
     ts(V("tmV", 0, 1), V("mkV", 0, 1), -1e25, None, OP.max)
     ts(V("mP"), V("mk", 0, 128), 0.5, 9.9e29, OP.subtract, OP.mult)
-    for d, n, w, c0, c in (("dL", 64, 1, -1e29, LIFT), ("dX", 64, 2, 1e29, -LIFT * EPS), ("dL2", 128, 1, -1e29, 128.0 * U), ("dL3", 256, 1, 1e29, -192.0)):
-        ts(V("mt", 0, n), V("mk", 0, n), c, None, OP.mult)
-        ts(V("mu", 0, n), V("mk", 0, n), c0, None, OP.mult)
-        copy(V(d, 0, 1), V("mu", 0, 1))
-        tt(V(d, w, n * w, w), V("mu", 1, n), V("mt", 0, n - 1), OP.add)
-    ts(V("dX", 1, 128, 2), V("mk", 0, 64), 512.0 * EPS, None, OP.mult)
+    for d, n, c0, c in (("dL", 64, -HUGE, LIFT), ("dL2", 128, -HUGE, 128.0 * U), ("dL3", 256, HUGE, -192.0)):
+        act(V("m" + d), V("mk", 0, n), AF.Copy, scale=c0)
+        fill(V("e" + d), c / c0)
+        scan(V(d), V("e" + d), V("m" + d), 0.0, OP.mult, OP.add)
+    fill(V("dX", 0, 36), 0.0)
+    ts(V("dX", 2, 34, 2), V("mk", 0, 16), -LIFT * EPS - 255.5 * EPS, None, OP.mult)
+    tt(V("dX", 0, 32, 2), V("dX", 0, 32, 2), V("mdL3", 0, 16), OP.add)
+    ts(V("dX", 1, 33, 2), V("mk", 0, 16), 1.0 + 512.0 * EPS, None, OP.mult)
+    fill(V("dX", 33, 34), -ROUND)
+    fill(V("dX", 34, 35), ROUND)
+    act(V("dX", 36, 72), V("dX", 0, 36), AF.Copy)
     quant(V("uq0"), V("us0"), V("ut"))
     do("v", lambda e: e.tensor_copy(T.uq[:, 0:128].bitcast(dt.uint32), T.uq0[:, 0:128].bitcast(dt.uint32).indirect(ap(UO))), [V("uq0"), UO], [V("uq")], 250)
     act(V("us"), V("us0", 0, 128), AF.Copy, l=UO)
@@ -361,7 +373,6 @@ def rank_program(g, core, T, topo):
     for m in range(8):
         act(V("rbt", 64 * m, 64 * m + 64), V("one"), AF.Copy, scale=V("c8", m, m + 1))
     select(V("idn"), [[-1, 128]], OP.is_equal, 0, 1)
-    iota(V("c1"), [[0, 8]], 0, 1)
     iota(V("jc"), [[2, 128]], 131072, 0)
     act(V("jc"), V("jc"), AF.Copy, scale=EPS)
     iota(V("ng", 16, 144), [[-1, 128]], 128, 0)
@@ -379,18 +390,18 @@ def rank_program(g, core, T, topo):
         o = (4, 4, 2, 2)[b]
         quant(V("eq", 128 * b, 128 * b + 128), V("es", 128 * b, 128 * b + 128), V(("et", "et1")[b % 2], o, o + 512))
     quant(V("rbq"), V("rbs"), V("rbt"))
-    bits(V("c2"), V("c1"), 15)
-    copy(V("cq"), V("c2"))
     for m in range(4):
-        ts(V("sm", m, m + 1), V("cq", 0, 1), U, (16.0 * m + 0.5) * U + BASE, OP.mult, OP.add)
+        act(V("sm", m, m + 1), V("cq", 0, 1), AF.Copy, scale=U, bias=(16.0 * m + 0.5) * U + BASE)
     ts(V("sm", 11, 12), V("cq", 0, 1), 15.0, None, OP.is_lt)
     for k, c, c0 in ((8, LIFT, 129.0), (9, -128.0, -1.0), (13, 192.0, -1.0), (14, -LIFT, 127.0), (15, 96.0, 0.0)):
-        ts(V("sm", k, k + 1), V("sm", 11, 12), c, c0, OP.mult, OP.add)
+        act(V("sm", k, k + 1), V("sm", 11, 12), AF.Copy, scale=c, bias=c0)
     ts(V("sm", 15, 16), V("cq", 0, 1), V("sm", 15, 16), 2.0, OP.add, OP.mult)
-    ts(V("cw"), V("cw"), V("sm", 15, 16), None, OP.add)
-    for v, c in ((V("A", 256, 257), 0.0), (V("nW", 0, 1), 1.0), (V("UL", 15, 16), 1.0), (V("UR", 1024, 1025), 1.0), (V("nkL", 128, 129), 0.0),
-                 (V("ng", 15, 16), 0.0), (V("Ct", 0, 1), BASE), (V("mB", 0, 2), 2.0 * U), (V("y", 0, 1), U)):
-        fill(v, c)
+    act(V("cw"), V("cw"), AF.Identity, bias=V("sm", 15, 16))
+    for n, a, b, c in (("A", 256, 257, 0), ("nW", 0, 1, 1), ("UL", 15, 16, 1), ("UL", 1040, 1041, 1), ("nkL", 128, 129, 0), ("nkR", 128, 129, -1),
+                       ("ng", 15, 16, 0), ("Ct", 0, 1, BASE), ("mB", 0, 2, 2 * U), ("y", 0, 1, U)):
+        level(n, a, b, int(c))
+    for h in range(4):
+        level("RP%d" % h, 224, 264, 0)
     level("FE", 0, 512, 0)
     level("F", 256, 512, 0)
     level("zt", 0, 512, 0)
@@ -442,6 +453,7 @@ def rank_program(g, core, T, topo):
         return V("TU", 512 * b + 256 + a, 512 * b + 256 + e)
 
     for t in range(R):
+        seen.clear()
         product("uq", "us", "X%d" % (t % 2), ("ps", "pst"))
         for h in range(2):
             act(V("Sw", 128 * h + 8, 128 * h + 136), V("pst", 512 * h, 512 * h + 128), AF.Copy)
@@ -459,50 +471,44 @@ def rank_program(g, core, T, topo):
             tt(V("nW", o + 1, o + 1 + e), V("ps%d" % h, 0, e), V("Sw", o + 10, o + 10 + e), OP.is_ge)
         for m in range(8):
             s = V("tsV", 32 * m + 31, 32 * m + 32)
-            if m < 2:
+            if m < NV:
                 ts(slot(m), V("VV"), s, None, OP.is_lt)
             else:
                 act(slot(m), V("VV"), AF.Sign, bias=s, scale=-1.0)
         scan(V("tmM"), V("M"), V("mP"), -4e29, OP.max, OP.min)
         scan(V("tsM"), V("rst"), V("tmM"), 0.0, OP.min, OP.max)
-        ts(V("As"), V("A", 0, 256, 2), EPS, None, OP.mult)
+        act(V("As"), V("A", 0, 256, 2), AF.Copy, scale=EPS)
         less(V("NJ"), V("As"), V("jc"))
         scan(V("dA"), V("dL3", 0, 128), V("A", 1, 256, 2), 0.0, OP.add, OP.min)
         tt(V("sm", 40, 48), V("dA", 15, 128, 16), V("cw"), OP.add)
         copy(PL, V("sm", 40, 48))
-        ts(V("sm", 48, 56), V("sm", 40, 48), EPS, 2.0 + 256.0 * EPS, OP.mult, OP.add)
+        act(V("sm", 48, 56), V("sm", 40, 48), AF.Copy, scale=EPS, bias=0.625 + 256.0 * EPS)
         for m in range(8):
-            s = V("tsM", 16 * m + 15, 16 * m + 16)
-            act(V("UL", 16 + 128 * m, 16 + 128 * m + 16 * m + 16), V("M", 0, 16 * m + 16), AF.Sign, bias=s, scale=-1.0)
-            r = V("UR", 128 * m + 16 * m, 128 * m + 128)
-            if m < 4:
-                ts(r, V("M", 16 * m, 128), s, None, OP.is_le)
-            else:
-                act(r, V("M", 16 * m, 128), AF.Sign, bias=s, scale=-1.0)
-                act(r, r, AF.Sign, bias=0.5)
+            act(V("UL", 16 + 128 * m, 144 + 128 * m), V("M"), AF.Sign, bias=V("tsM", 16 * m + 15, 16 * m + 16), scale=-1.0)
         ranks((0, 1))
         tt(V("nkL", 0, 128), P, V("NJ"), OP.subtract)
+        act(V("nkR", 0, 128), V("nkL", 0, 128), AF.Copy, bias=-1.0)
         act(V("A2", 0, 257), V("A", 0, 257), AF.Copy, bias=512.0, scale=256.0)
         less(V("du"), V("A2", 0, 256), V("A2", 1, 257))
         scan(V("hpx"), V("par"), V("du"), 0.0, OP.mult, OP.max)
-        ts(V("hp"), V("hpx", 1, 256, 2), 8e26, -1e27, OP.mult, OP.add)
+        act(V("hp"), V("hpx", 1, 256, 2), AF.Copy, scale=8e26, bias=-1e27)
         scan(V("PK"), V("hp"), V("M"), 0.0, OP.add, OP.min)
         for b in range(4):
             act(Tf(b), V("pst", 512 * b, 512 * b + 256), AF.Copy)
             act(V("BI", 256 * b, 256 * b + 256, 2), Tf(b), AF.Copy, scale=0.5, l=PL)
         for m in range(7, -1, -1):
-            k, o = 16 * m + 15 + (m == 0), 80 + 16 * (m % 4)
-            scan(V("RP%d" % (m // 4), 2 * (o - k) + 1, 2 * o, 2), V("UL", 144 * m + 31 - k, 144 * m + 31), V("nkL", 16 * m + 16 - k, 16 * m + 16),
+            k, o = 16 * m + 15 + (m == 0), 224 + 36 * (m % 2)
+            scan(V("RP%d" % (m // 2), o - 2 * k + 1, o, 2), V("UL", 144 * m + 31 - k, 144 * m + 31), V("nkL", 16 * m + 16 - k, 16 * m + 16),
                  V("sm", 48 + m, 49 + m), OP.mult, OP.max)
         for m in range(8):
-            a, e, o = 16 * m, 127 + m // 7, 64 + 16 * (m % 4)
-            scan(V("RP%d" % (m // 4), 2 * (o + e - 1 - a), 2 * o - 1, -2), V("UR", 128 * m + e, 128 * m + a, -1), V("nkL", e, a, -1),
-                 V("sm", 48 + m, 49 + m), OP.mult, OP.max)
-        for h in range(2):
-            scan(V("tR", 128 * h, 128 * h + 128), V("dX"), V("RP%d" % h, 128, 256), 0.0, OP.add, OP.min)
-        ts(V("k8"), V("tR", 31, 256, 32), 1.0 / EPS, LIFT, OP.mult, OP.add)
-        bits(V("l8"), V("k8"), 511)
-        copy(LI, V("l8"))
+            a, e, o = 16 * m, 127 + m // 7, 192 + 36 * (m % 2)
+            scan(V("RP%d" % (m // 2), o + 2 * (e - 1 - a), o - 1, -2), V("UL", 16 + 128 * m + e, 16 + 128 * m + a, -1), V("nkR", e, a, -1),
+                 -0.25, OP.min, OP.max)
+        for h in range(4):
+            scan(V("tR", 72 * h, 72 * h + 72), V("dX"), V("RP%d" % h, 192, 264), 0.0, OP.add, OP.min)
+        tt(V("d8"), V("tR", 32, 288, 36), V("tR", 34, 288, 36), OP.subtract)
+        ts(LI, V("d8"), 1.0 / EPS, 255.5, OP.mult, OP.add)
+        ts(V("k8"), V("tR", 32, 288, 36), 1.0 / EPS, LIFT + 255.5, OP.mult, OP.add)
         tt(V("np"), V("Sw", 8, 520), V("PK"), OP.subtract, l=LI)
         bits(V("q8"), V("k8"), 255)
         copy(LQ, V("q8"))
@@ -513,7 +519,7 @@ def rank_program(g, core, T, topo):
         scan(V("tsN", 127, -1, -1), V("rst"), V("tmN", 127, -1, -1), 0.0, OP.min, OP.max)
         for m in range(8):
             s = V("tsN", 16 * m, 16 * m + 1)
-            if m < 5:
+            if m < NS:
                 act(slot(m, 16 * m, 128), V("np", 16 * m, 128), AF.Relu, bias=s, scale=-1.0)
                 act(slot(m, 16 * m, 128), slot(m, 16 * m, 128), AF.Sign)
             else:
@@ -525,14 +531,14 @@ def rank_program(g, core, T, topo):
         ts(V("npk"), V("du"), 0.5, U, OP.is_lt, OP.mult)
         scan(V("ni"), V("npk"), V("npk"), 0.0, OP.add, OP.max)
         ts(V("sm", 10, 11), V("ni", 255, 256), -192.0 * U, 0.0, OP.add, OP.max)
-        ts(V("sm", 12, 13), V("sm", 10, 11), 1024.0 * EPS / U, 65.0 * 1024.0 * EPS, OP.mult, OP.add)
+        act(V("sm", 12, 13), V("sm", 10, 11), AF.Copy, scale=1024.0 * EPS / U, bias=65.0 * 1024.0 * EPS)
         ts(V("mB", 2, 258), V("ni"), V("sm", 10, 11), 2.0 * U, OP.min, OP.add)
         less(V("ph"), V("mB", 2, 258, 2), V("mB", 0, 256, 2))
         less(V("fl"), V("mB", 2, 66), V("mB", 1, 65))
-        ts(V("pf"), V("fl"), -2.0, 256.0, OP.mult, OP.add)
+        act(V("pf"), V("fl"), AF.Copy, scale=-2.0, bias=256.0)
         less(V("fx"), V("fv"), V("pf"))
         dscan(V("fw"), V("fx"), V("dL"))
-        ts(V("sm", 20, 24), V("fw", 15, 64, 16), V("sm", 14, 15), None, OP.add)
+        act(V("sm", 20, 24), V("fw", 15, 64, 16), AF.Identity, bias=V("sm", 14, 15))
         ts(V("sm", 24, 28), V("sm", 20, 24), 128.0, None, OP.is_lt)
         tt(V("sm", 28, 32), V("sm", 20, 24), V("b0"), OP.max)
         for m in range(7, -1, -1):
@@ -541,7 +547,7 @@ def rank_program(g, core, T, topo):
                  OP.max)
         for h in range(2):
             dscan(V("tNP", 64 * h, 64 * h + 64), V("NP%d" % h, 64, 128), V("dL"))
-        ts(V("sm", 32, 40), V("tNP", 15, 128, 16), -1.0, V("sm", 8, 9), OP.mult, OP.add)
+        act(V("sm", 32, 40), V("tNP", 15, 128, 16), AF.Identity, scale=-1.0, bias=V("sm", 8, 9))
         copy(NL, V("sm", 32, 40))
         bits(V("s8"), V("k8"), 768)
         tt(V("sm", 56, 64), V("sm", 32, 40), V("s8"), OP.subtract)
@@ -551,8 +557,8 @@ def rank_program(g, core, T, topo):
         act(V("nW2"), V("nW"), AF.Copy, bias=512.0, scale=256.0)
         less(V("d0"), V("nW2"), V("A2", 0, 256))
         scan(V("F1"), V("d0"), V("sv"), 0.0, OP.min, OP.max)
-        ts(V("u1"), V("F1"), 0.0, None, OP.is_le)
-        scan(V("h1", 255, -1, -1), V("u1", 255, -1, -1), V("F1", 255, -1, -1), 0.0, OP.mult, OP.max)
+        act(V("u1"), V("F1"), AF.Copy, scale=-256.0, bias=256.0)
+        scan(V("h1", 255, -1, -1), V("u1", 255, -1, -1), V("F1", 255, -1, -1), 0.0, OP.min, OP.max)
         scan(V("t1"), V("dL3"), V("h1"), 0.0, OP.add, OP.min)
         ts(CL, V("t1", 15, 256, 16), V("sm", 13, 14), None, OP.add)
         ts(V("K"), P, V("sm", 12, 13), U, OP.is_ge, OP.mult)
@@ -570,7 +576,7 @@ def rank_program(g, core, T, topo):
         send(t)
         scan(V("Cm"), V("K"), V("ph"), BASE - U, OP.add, OP.add)
         tt(V("y", 1, 129), V("Ct", 0, 129), V("Cm"), OP.subtract, l=NL)
-        ts(V("pK"), V("K"), -128.0, 128.0 * U, OP.mult, OP.add)
+        act(V("pK"), V("K"), AF.Copy, scale=-128.0, bias=128.0 * U)
         less(V("Kc"), Cn, V("pK"))
         tt(V("bw"), V("Ct", 0, 129), V("Kc"), OP.max, l=N3)
         ts(V("pen"), V("y", 1, 129), 256.0, BASE, OP.mult, OP.max)
@@ -616,7 +622,7 @@ def rank_program(g, core, T, topo):
     dma("a", T.oc[:, :], T.XQ[:, :].bitcast(dt.uint8), [XQ], [])
     for k in range(4):
         dma("a" if k % 2 else "s", T.osc[4 * k:4 * k + 4, :], T.XS[32 * k:32 * k + 4, :], [XS], [])
-    copy(V("yb", 0, 128), V("ps0", 0, 128))
+    act(V("yb", 0, 128), V("ps0", 0, 128), AF.Copy)
     copy(V("yb", 128, 256), V("ps1", 0, 128))
     dma("s", T.y[:, :], T.yb[:, :], [V("yb")], [])
     issue()

@@ -7,29 +7,32 @@ C, K, R = 256, 64, 3
 STEP = [1, 2, 4]
 F32, B16, I32, U16, U8, MX = "float32", "bfloat16", "int32", "uint16", "uint8", "float8_e4m3fn_x4"
 EPS = 2.0 ** -19
-LIFT, HUGE, ROUND = 2.0 ** 21, 2.0 ** 96, 1.5 * 2.0 ** 13
+LIFT, HUGE, ROUND = 2.0 ** 21, 2.0 ** 96, 3 * 2 ** 13
 U = 128.0
 BASE = 64.0 * U
-CYCLE, FIXED, WAKE, NET = 0.83, 0.0, 220.0, 2500.0
-CASES = ((1.0, 190.0, 3500.0), (1.0, 240.0, 2500.0), (1.25, 210.0, 2500.0))
-TRIES, ALIKE, SEED = 7000, 0.7, 0
+CYCLE, FIXED, WAKE, NET, COPY = 0.83, 0.0, 230.0, 1600.0, 1800.0
+CASES = ((1.0, 240.0, 1300.0), (1.0, 210.0, 2300.0), (1.3, 220.0, 1600.0))
+TRIES, ALIKE, SEED, MOVES, HEAT = 300, 1.0, 0, 45000, 30.0
+GT, HV, TM, HC = True, 1, True, 1
+PICKS = ((0, 0, 128, "v"), (1, 0, 128, "v"), (2, 0, 128, "a"), (3, 0, 128, "a"), (0, 128, 256, "v"), (1, 128, 256, "a"), (2, 128, 256, "a"),
+         (3, 128, 256, "a"))
 NV, NS = 2, 5
 ORDERS = {}
 
 _SB = {
-    F32: {"sm": 64, "c8": 8, "Sw": 528, "M": 128, "VV": 128, "PK": 128, "tmV": 256,
-          "tmM": 128, "tmN": 128, "tsV": 256, "tsM": 128, "tsN": 128, "tR": 288, "d8": 8, "tNP": 128, "NJ": 128, "nkL": 136, "nkR": 136, "RP0": 464, "RP1": 400, "RP2": 336, "RP3": 272,
-          "np": 128, "s64": 64, "H": 256, "G3": 640, "out": 256, "yb": 256, "ka": 128, "kc": 128, "fw": 64},
-    B16: {"X0": 1024, "X1": 1024, "ut": 512, "vt": 512, "et": 520, "et1": 520, "rbt": 512, "zt": 512, "one": 64, "idn": 128, "A": 272, "A2": 272,
-          "du": 256, "hpx": 256, "hp": 128, "FV": 1024, "FE": 512, "UL": 1056, "ed": 416, "F": 512, "TU": 2048, "BI": 1024,
+    F32: {"sm": 64, "c8": 8, "Sw": 776, "M": 128, "VV": 128, "PK": 128, "PKm": 128, "tmV": 256,
+          "tmM": 128, "tmN": 128, "tsV": 256, "tsM": 128, "tsN": 128, "tR": 288, "d8": 8, "s8": 8, "tNP": 128, "NJ": 128, "nkL": 136, "nkR": 136, "RP0": 464, "RP1": 400, "RP2": 336, "RP3": 272,
+          "np": 128, "s64": 64, "H": 256, "G3": 1024, "out": 256, "yb": 256, "ka": 128, "kc": 128, "fw": 64},
+    B16: {"X0": 1024, "X1": 1024, "ut": 512, "vt": 512, "et": 520, "et1": 520, "rbt": 512, "one": 64, "idn": 128, "A": 272, "A2": 272,
+          "du": 256, "hpx": 256, "hp": 128, "FV": 1024, "FE": 512, "UL": 1056, "ed": 416, "F": 512, "TU": 4096, "BI": 1024,
           "Ct": 144, "HT": 192, "colT": 320, "hc": 256, "NP0": 128, "NP1": 128},
     U16: {"su": 96},
-    MX: {"uq0": 128, "uq": 128, "vq": 128, "wq": 512, "eq": 512, "rbq": 128, "zq": 128, "FVq": 256, "FEq": 128, "XQ": 256},
-    U8: {"us0": 128, "us": 128, "vs": 128, "wp": 512, "es": 512, "rbs": 128, "zs": 128, "FVs": 256, "FEs": 128, "XS": 256},
+    MX: {"uq0": 128, "uq": 128, "vq": 128, "wq": 512, "eq": 512, "rbq": 128, "FVq": 256, "FEq": 128, "XQ": 256},
+    U8: {"us0": 128, "us": 128, "vs": 128, "wp": 512, "es": 512, "rbs": 128, "FVs": 256, "FEs": 128, "XS": 256},
 }
 for _t in range(R):
-    for _n, _d in (("Fq", MX), ("Fs", U8), ("lc", MX), ("ls", U8)):
-        _SB[_d]["%s%d" % (_n, _t)] = 128
+    for _n, _d in (("Fq", MX), ("Fs", U8)):
+        _SB[_d]["%s%d" % (_n, _t)] = 192
 _JOINT = {
     "kf": (F32, {"jc": 128, "cq": 8, "cw": 8, "b0": 4, "dX": 72}),
     "kb": (B16, {"mk": 256, "par": 256, "ng": 144, "mP": 128, "rst": 128, "mkV": 256, "rstV": 256, "dL": 64, "dL2": 128, "dL3": 256,
@@ -39,7 +42,6 @@ _JOINT = {
                  "d0": 256, "F1": 256, "u1": 256, "h1": 256, "t1": 256}),
     "rb": (B16, {"K": 128, "pK": 128, "Cm": 128, "Kc": 128, "y": 129, "bw": 128, "pen": 128, "bv": 128, "gl": 128, "vl": 128, "u2": 128,
                  "tsb": 256}),
-    "l8s": (I32, {"k8": 8, "q8": 8, "s8": 8}),
 }
 WIDTH = {n: w for l in _SB.values() for n, w in l.items()}
 TYPE = {n: d for d, l in _SB.items() for n in l}
@@ -51,11 +53,11 @@ for _b, (_d, _l) in _JOINT.items():
         PLACE[_n], WIDTH[_n], TYPE[_n] = (_b, _o), _w, _d
         _o += (_w + 31) // 32 * 32
     SCRATCH[_b] = ("sbuf", [128, _o], _d)
-_PS = ("ps0", "ps1", "psr", "pst")
+_PS = ("ps0", "ps1", "psr", "psx", "pst")
 for _n in _PS:
     SCRATCH[_n] = ("psum", [128, 2048 if _n == "pst" else 512], F32)
     TYPE[_n] = F32
-SEMAPHORES = ["qv", "qa", "qt", "qg"] + ["d%d" % i for i in range(48)] + ["arr%d" % t for t in range(R)] + ["snt"]
+SEMAPHORES = ["qv", "qa", "qt", "qg"] + ["d%d" % i for i in range(40)] + ["%s%d%d" % (n, t, k) for n in ("arr", "snt") for t in range(R) for k in range(1)]
 
 
 def planner(g, T):
@@ -149,8 +151,8 @@ def planner(g, T):
         for f, wake, net in CASES:
             pre = [[(j, wake if w else 0.0) for j, w in o["pre"].items()] for o in ops]
             sent = [o["cost"] == NET for o in ops]
-            c = [net if s else x if x > 2000.0 else f * x for s, x in zip(sent, cost)]
-            cases.append((pre, c, [net if s and h else h if x > 2000.0 else f * h for s, x, h in zip(sent, cost, hold)]))
+            c = [net if s else x if x > 1200.0 else f * x for s, x in zip(sent, cost)]
+            cases.append((pre, c, [h if x > 1200.0 else f * h for x, h in zip(cost, hold)]))
 
         def judge(out):
             total = 0.0
@@ -186,7 +188,83 @@ def planner(g, T):
             least, end = min(least, end), judge(out)
             if best is None or end <= best[0]:
                 best = (end, out, noise, patience)
-        return best[1]
+
+        (p0, c0, h0), (p1, c1, h1), (p2, c2, h2) = cases
+        edges = [[(j, a[1], b[1], c[1]) for (j, a, b, c) in zip([x[0] for x in p0[i]], p0[i], p1[i], p2[i])] for i in range(n)]
+        after = [[k for k, w in succ[i]] for i in range(n)]
+        twins = {}
+        for i, o in enumerate(ops):
+            twins.setdefault(o["like"], []).append(i)
+        turn = {i: k for l in twins.values() for k, i in enumerate(l)}
+
+        def run(lines):
+            left, nxt = need[:], [-1] * n
+            for l in lines:
+                for a, b in zip(l, l[1:]):
+                    nxt[a] = b
+                    left[b] += 1
+            s0, s1, s2, f0, f1, f2 = [0.0] * n, [0.0] * n, [0.0] * n, [0.0] * n, [0.0] * n, [0.0] * n
+            out = [i for i in range(n) if not left[i]]
+            for i in out:
+                a, b, c = s0[i], s1[i], s2[i]
+                for j, u, v, w in edges[i]:
+                    x = f0[j] + u
+                    if x > a:
+                        a = x
+                    x = f1[j] + v
+                    if x > b:
+                        b = x
+                    x = f2[j] + w
+                    if x > c:
+                        c = x
+                s0[i], s1[i], s2[i] = a, b, c
+                f0[i], f1[i], f2[i] = a + c0[i], b + c1[i], c + c2[i]
+                k = nxt[i]
+                if k >= 0:
+                    s0[k], s1[k], s2[k] = a + h0[i], b + h1[i], c + h2[i]
+                    left[k] -= 1
+                    if not left[k]:
+                        out.append(k)
+                for k in after[i]:
+                    left[k] -= 1
+                    if not left[k]:
+                        out.append(k)
+            if len(out) < n:
+                return None
+            return max(f0) + max(f1) + max(f2), out, ((s0, f0), (s1, f1), (s2, f2))
+
+        def held(lines, times):
+            prev, pairs = {b: a for l in lines for a, b in zip(l, l[1:])}, []
+            for (s, f), (pre, c, h) in zip(times, cases):
+                i = max(range(n), key=lambda x: f[x])
+                while s[i] > 0.0:
+                    j = next((j for j, w in pre[i] if f[j] + w >= s[i] - 1e-6), None)
+                    if j is None:
+                        j = prev[i]
+                        pairs.append((j, i))
+                    i = j
+            return pairs
+
+        lines = [[i for i in best[1] if qs[i] == q] for q in range(len(names))]
+        now = top = run(lines)
+        pairs = held(lines, now[2])
+        for k in range(MOVES):
+            j, i = pairs[int(rng.integers(len(pairs)))]
+            far, back, both = int(rng.integers(1, 5)) if k % 2 else 1, k % 4 < 2, k % 3 and len(twins[ops[i]["like"]]) == len(twins[ops[j]["like"]])
+            l = lines[qs[i]][:]
+            for a, b in zip(twins[ops[j]["like"]], twins[ops[i]["like"]]) if both else [(j, i)]:
+                x, y = l.index(a), l.index(b)
+                if x < y and back:
+                    l.insert(max(0, x - far + 1), l.pop(y))
+                elif x < y:
+                    l.insert(y + far - 1, l.pop(x))
+            new = lines[:qs[i]] + [l] + lines[qs[i] + 1:]
+            r = run(new)
+            if r and r[0] <= now[0] + HEAT * (1.0 - k / MOVES) * rng.exponential():
+                lines, now, pairs = new, r, held(new, r[2])
+                if r[0] < top[0]:
+                    top = r
+        return top[1]
 
     def issue():
         key = str([(o["q"], o["cost"], sorted(o["pre"].items())) for o in ops])
@@ -260,10 +338,10 @@ def rank_program(g, core, T, topo):
     def do(q, call, reads, writes, cycles, adds=False):
         add(q, lambda e: call(e).then_inc(T.sem["q" + q], 1), reads, writes, max(64, cycles) * CYCLE + FIXED, adds=adds)
 
-    def dma(q, out, in_, reads, writes):
+    def dma(q, out, in_, reads, writes, cost=COPY):
         s = "d%d" % nd[0]
         nd[0] += 1
-        add(q, lambda e: e.dma_start(out, in_).then_inc(T.sem[s], 16), reads, writes, 2501.0, 100.0, s, 16)
+        add(q, lambda e: e.dma_start(out, in_).then_inc(T.sem[s], 16), reads, writes, cost, 100.0, s, 16)
 
     def tt(out, a, b, op, l=None):
         n = width(out)
@@ -327,9 +405,9 @@ def rank_program(g, core, T, topo):
         scan(out, a, b, 0.0, OP.max, OP.subtract)
 
     LI, EL, NL, HL, UO = V("su", 0, 8), V("su", 8, 12), V("su", 16, 24), V("su", 24, 40), V("su", 40, 48)
-    PL, LQ, N3, CL = V("su", 48, 56), V("su", 56, 64), V("su", 64, 72), V("su", 72, 88)
+    PL, N3, CL = V("su", 48, 56), V("su", 64, 72), V("su", 72, 88)
 
-    dma("s", ap(V("X0")), T.x[:, :], [], [V("X0")])
+    dma("s", ap(V("X0")), T.x[:, :], [], [V("X0")], 1.4 * COPY)
     dma("a", ap(V("ut")), T.u[:, :], [], [V("ut")])
     dma("s", ap(V("wq")).bitcast(dt.uint8), T.wc[:, :], [V("X0"), V("ut")], [V("wq")])
     dma("s", ap(V("wp")), T.ws[:, :], [V("X0"), V("ut")], [V("wp")])
@@ -346,21 +424,21 @@ def rank_program(g, core, T, topo):
         fill(V(n, 0, w), c)
         fill(V(n, 0, w, k), c0)
     fill(V("Sw", 0, 8), -1e25)
-    fill(V("Sw", 264, 528), -1e25)
+    act(V("Sw", 264, 520), V("mt"), AF.Copy, scale=0.0, bias=-1e25)
     for p in range(2):
         ts(V("mkV", p, 256, 2), V("mk", 0, 128), 0.5, -9.9e29, OP.subtract, OP.mult)
     ts(V("tmV", 0, 1), V("mkV", 0, 1), -1e25, None, OP.max)
-    ts(V("mP"), V("mk", 0, 128), 0.5, 9.9e29, OP.subtract, OP.mult)
+    act(V("mP"), V("mkV", 0, 256, 2), AF.Copy, scale=-1.0)
     for d, n, c0, c in (("dL", 64, -HUGE, LIFT), ("dL2", 128, -HUGE, 128.0 * U), ("dL3", 256, HUGE, -192.0)):
         act(V("m" + d), V("mk", 0, n), AF.Copy, scale=c0)
         fill(V("e" + d), c / c0)
         scan(V(d), V("e" + d), V("m" + d), 0.0, OP.mult, OP.add)
     fill(V("dX", 0, 36), 0.0)
-    ts(V("dX", 2, 34, 2), V("mk", 0, 16), -LIFT * EPS - 255.5 * EPS, None, OP.mult)
+    act(V("dX", 2, 34, 2), V("mk", 0, 16), AF.Copy, scale=-LIFT * EPS - 511.5 * EPS)
     tt(V("dX", 0, 32, 2), V("dX", 0, 32, 2), V("mdL3", 0, 16), OP.add)
-    ts(V("dX", 1, 33, 2), V("mk", 0, 16), 1.0 + 512.0 * EPS, None, OP.mult)
-    fill(V("dX", 33, 34), -ROUND)
-    fill(V("dX", 34, 35), ROUND)
+    act(V("dX", 1, 33, 2), V("mk", 0, 16), AF.Copy, scale=1.0 + 512.0 * EPS)
+    level("dX", 33, 34, -ROUND)
+    level("dX", 34, 35, ROUND)
     act(V("dX", 36, 72), V("dX", 0, 36), AF.Copy)
     quant(V("uq0"), V("us0"), V("ut"))
     do("v", lambda e: e.tensor_copy(T.uq[:, 0:128].bitcast(dt.uint32), T.uq0[:, 0:128].bitcast(dt.uint32).indirect(ap(UO))), [V("uq0"), UO], [V("uq")], 250)
@@ -404,28 +482,21 @@ def rank_program(g, core, T, topo):
         level("RP%d" % h, 224, 264, 0)
     level("FE", 0, 512, 0)
     level("F", 256, 512, 0)
-    level("zt", 0, 512, 0)
-    quant(V("zq"), V("zs"), V("zt"))
-    for t in range(R):
-        dma("s", T["lc%d" % t][:, 64:128].bitcast(dt.uint8), T.zq[:, 64:128].bitcast(dt.uint8), [V("zq")], [V("lc%d" % t, 64, 128)])
-        dma("s", T["ls%d" % t][:, 64:128], T.zs[:, 64:128], [V("zs")], [V("ls%d" % t, 64, 128)])
     quant(V("vq"), V("vs"), V("vt"))
 
-    far = [T.cores[rank ^ s] for s in STEP]
-    engs = topo.engines(core, far[1])
-    mask = 0
-    for e in engs:
-        mask |= 1 << e
-
-    def send(t):
-        rid, pid, _ = topo.addr(far[t])
-        arr = T.sem["arr%d" % t]
+    def send(t, k, pairs, cost):
+        far = T.cores[rank ^ STEP[t]]
+        rid, pid, _ = topo.addr(far)
+        mask = topo.mask(core, T.cores[rank ^ STEP[-1]])
+        n = len(pairs) * len(topo.engines(core, T.cores[rank ^ STEP[-1]]))
+        arr, snt = "arr%d%d" % (t, k), "snt%d%d" % (t, k)
 
         def call(e):
-            e.remote_dma(T["lc%d" % t][:, 0:64].bitcast(dt.uint8), T["Fq%d" % t][:, 0:64].bitcast(dt.uint8), arr, T.sem.snt, pid, rid, mask)
-            e.remote_dma(T["ls%d" % t][:, 0:64], T["Fs%d" % t][:, 0:64], arr, T.sem.snt, pid, rid, mask)
-        add("g", call, [V("Fq%d" % t), V("Fs%d" % t)], [], NET, NET, "snt", 2 * len(engs))
-        add("in", None, [V("Fq%d" % t)], [V("lc%d" % t, 0, 64), V("ls%d" % t, 0, 64)], NET, 0.0, "arr%d" % t, 2 * len(engs))
+            for a, b in pairs:
+                a, b = [ap(x).bitcast(dt.uint8) if TYPE[x[0]] == MX else ap(x) for x in (a, b)]
+                e.remote_dma(b, a, T.sem[arr], T.sem[snt], pid, rid, mask)
+        add("g", call, [a for a, b in pairs], [], cost, 300.0 * len(pairs), snt, n)
+        add("in", None, [a for a, b in pairs], [b for a, b in pairs], cost, 0.0, arr, n)
 
     XQ, XS, P = V("XQ"), V("XS"), V("psr", 0, 128)
     Cn = V("Ct", 1, 129)
@@ -450,7 +521,7 @@ def rank_program(g, core, T, topo):
         return V("FV", o + 4 * a, 512 * (m // 4) + 4 * b, 4)
 
     def Tf(b, a=0, e=256):
-        return V("TU", 512 * b + 256 + a, 512 * b + 256 + e)
+        return V("TU", 1024 * b + 256 + a, 1024 * b + 256 + e)
 
     for t in range(R):
         seen.clear()
@@ -461,9 +532,13 @@ def rank_program(g, core, T, topo):
             mm(V("pst", 512 * b, 512 * b + 256), V("eq", 128 * b, 128 * b + 128), V("es", 128 * b, 128 * b + 128), XQ, XS)
         for h in range(2):
             S, o, e = "ps%d" % h, 128 * h, 128 - h
-            tt(V("tmV", o + 1, o + 1 + e), V(S, 0, e), V("mkV", o + 1, o + 1 + e), OP.max)
             tt(V("VV", o // 2, o // 2 + 64), V(S, 0, 128, 2), V("Sw", o + 7, o + 135, 2), OP.min)
-            scan(V("tsV", o, o + 128), V("rstV", o, o + 128), V("tmV", o, o + 128), 0.0, OP.max, OP.min)
+            if TM:
+                tt(V("tmV", o + 1, o + 1 + e), V(S, 0, e), V("mkV", o + 1, o + 1 + e), OP.max)
+                scan(V("tsV", o, o + 128), V("rstV", o, o + 128), V("tmV", o, o + 128), 0.0, OP.max, OP.min)
+            elif h:
+                scan(V("tmV", 128, 256), V("VV"), V("mP"), -4e29, OP.max, OP.min)
+                scan(V("tsV", 1, 256, 2), V("rst"), V("tmV", 128, 256), 0.0, OP.min, OP.max)
             tt(V("M", o // 2, o // 2 + 64), V(S, 0, 128, 2), V("Sw", o + 9, o + 137, 2), OP.max)
             tt(V("A", o, o + 128), V(S, 0, 128), V("Sw", o + 7, o + 135), OP.is_gt)
         for h in range(2):
@@ -477,6 +552,7 @@ def rank_program(g, core, T, topo):
                 act(slot(m), V("VV"), AF.Sign, bias=s, scale=-1.0)
         scan(V("tmM"), V("M"), V("mP"), -4e29, OP.max, OP.min)
         scan(V("tsM"), V("rst"), V("tmM"), 0.0, OP.min, OP.max)
+        dma("s", T.Sw[:, 520:776], T.Sw[:, 8:264], [V("Sw", 8, 264)], [V("Sw", 520, 776)])
         act(V("As"), V("A", 0, 256, 2), AF.Copy, scale=EPS)
         less(V("NJ"), V("As"), V("jc"))
         scan(V("dA"), V("dL3", 0, 128), V("A", 1, 256, 2), 0.0, OP.add, OP.min)
@@ -495,6 +571,8 @@ def rank_program(g, core, T, topo):
         scan(V("PK"), V("hp"), V("M"), 0.0, OP.add, OP.min)
         for b in range(4):
             act(Tf(b), V("pst", 512 * b, 512 * b + 256), AF.Copy)
+            for a in (256, 512):
+                dma("s", ap(Tf(b, a, a + 256)), ap(Tf(b)), [Tf(b)], [Tf(b, a, a + 256)])
             act(V("BI", 256 * b, 256 * b + 256, 2), Tf(b), AF.Copy, scale=0.5, l=PL)
         for m in range(7, -1, -1):
             k, o = 16 * m + 15 + (m == 0), 224 + 36 * (m % 2)
@@ -507,15 +585,16 @@ def rank_program(g, core, T, topo):
         for h in range(4):
             scan(V("tR", 72 * h, 72 * h + 72), V("dX"), V("RP%d" % h, 192, 264), 0.0, OP.add, OP.min)
         tt(V("d8"), V("tR", 32, 288, 36), V("tR", 34, 288, 36), OP.subtract)
-        ts(LI, V("d8"), 1.0 / EPS, 255.5, OP.mult, OP.add)
-        ts(V("k8"), V("tR", 32, 288, 36), 1.0 / EPS, LIFT + 255.5, OP.mult, OP.add)
-        tt(V("np"), V("Sw", 8, 520), V("PK"), OP.subtract, l=LI)
-        bits(V("q8"), V("k8"), 255)
-        copy(LQ, V("q8"))
+        ts(LI, V("d8"), 1.0 / EPS, 511.5, OP.mult, OP.add)
+        tt(V("np"), V("Sw", 8, 776), V("PK"), OP.subtract, l=LI)
         for b in range(4):
-            act(V("BI", 256 * b + 1, 256 * b + 256, 2), Tf(b), AF.Copy, scale=0.5, l=LQ)
-            scan(V("TU", 512 * b, 512 * b + 256), V("par"), V("BI", 256 * b, 256 * b + 256), 0.0, OP.mult, OP.add)
-        scan(V("tmN"), V("np"), V("mP"), -4e29, OP.max, OP.min)
+            act(V("BI", 256 * b + 1, 256 * b + 256, 2), Tf(b, 0, 768), AF.Copy, scale=0.5, l=LI)
+            scan(V("TU", 1024 * b, 1024 * b + 256), V("par"), V("BI", 256 * b, 256 * b + 256), 0.0, OP.mult, OP.add)
+        if GT:
+            scan(V("PKm"), V("PK"), V("mkV", 0, 256, 2), 4e29, OP.min, OP.max)
+            tt(V("tmN"), V("Sw", 8, 776), V("PKm"), OP.subtract, l=LI)
+        else:
+            scan(V("tmN"), V("np"), V("mP"), -4e29, OP.max, OP.min)
         scan(V("tsN", 127, -1, -1), V("rst"), V("tmN", 127, -1, -1), 0.0, OP.min, OP.max)
         for m in range(8):
             s = V("tsN", 16 * m, 16 * m + 1)
@@ -528,9 +607,10 @@ def rank_program(g, core, T, topo):
                 ts(slot(m, 0, 16 * m), V("np", 0, 16 * m), s, None, OP.is_le)
         tt(V("FE", 0, 512, 4), V("np"), V("tsN"), OP.is_equal)
         ranks((2, 1, 0))
-        ts(V("npk"), V("du"), 0.5, U, OP.is_lt, OP.mult)
+        act(V("npk"), V("du"), AF.Relu)
+        act(V("npk"), V("npk"), AF.Copy, scale=-U / 256.0, bias=U)
         scan(V("ni"), V("npk"), V("npk"), 0.0, OP.add, OP.max)
-        ts(V("sm", 10, 11), V("ni", 255, 256), -192.0 * U, 0.0, OP.add, OP.max)
+        act(V("sm", 10, 11), V("ni", 255, 256), AF.Relu, bias=-192.0 * U)
         act(V("sm", 12, 13), V("sm", 10, 11), AF.Copy, scale=1024.0 * EPS / U, bias=65.0 * 1024.0 * EPS)
         ts(V("mB", 2, 258), V("ni"), V("sm", 10, 11), 2.0 * U, OP.min, OP.add)
         less(V("ph"), V("mB", 2, 258, 2), V("mB", 0, 256, 2))
@@ -549,7 +629,7 @@ def rank_program(g, core, T, topo):
             dscan(V("tNP", 64 * h, 64 * h + 64), V("NP%d" % h, 64, 128), V("dL"))
         act(V("sm", 32, 40), V("tNP", 15, 128, 16), AF.Identity, scale=-1.0, bias=V("sm", 8, 9))
         copy(NL, V("sm", 32, 40))
-        bits(V("s8"), V("k8"), 768)
+        act(V("s8"), V("d8"), AF.Relu, scale=512.0 / EPS, bias=256.0 * 512.0)
         tt(V("sm", 56, 64), V("sm", 32, 40), V("s8"), OP.subtract)
         copy(N3, V("sm", 56, 64))
         less(V("sv"), V("pv"), V("npk"))
@@ -569,11 +649,11 @@ def rank_program(g, core, T, topo):
             ts(V("su", 8 + m, 9 + m), V("sm", 16 + m, 17 + m), V("sm", 24 + m, 25 + m), V("sm", 28 + m, 29 + m), OP.mult, OP.add)
         for b in range(4):
             if b % 2:
-                act(V("F", b, 256, 4), V("TU", 512 * b, 512 * b + 320), AF.Copy, l=EL)
+                act(V("F", b, 256, 4), V("TU", 1024 * b, 1024 * b + 320), AF.Copy, l=EL)
             else:
-                copy(V("F", b, 256, 4), V("TU", 512 * b, 512 * b + 320), l=EL)
-        quant(V("Fq%d" % t), V("Fs%d" % t), V("F"))
-        send(t)
+                copy(V("F", b, 256, 4), V("TU", 1024 * b, 1024 * b + 320), l=EL)
+        quant(V("Fq%d" % t, 0, 128), V("Fs%d" % t, 0, 128), V("F"))
+        send(t, 0, [(V(n % t, 0, 64), V(n % t, 128, 192)) for n in ("Fq%d", "Fs%d")], NET)
         scan(V("Cm"), V("K"), V("ph"), BASE - U, OP.add, OP.add)
         tt(V("y", 1, 129), V("Ct", 0, 129), V("Cm"), OP.subtract, l=NL)
         act(V("pK"), V("K"), AF.Copy, scale=-128.0, bias=128.0 * U)
@@ -588,8 +668,8 @@ def rank_program(g, core, T, topo):
         ts(V("u2"), V("vl"), 0.0, None, OP.is_equal)
         scan(V("HT", 127, -1, -1), V("u2", 127, -1, -1), V("vl", 127, -1, -1), 0.0, OP.mult, OP.add)
         for h in range(2):
-            if h:
-                act(V("hc", 128, 256), V("HT"), AF.Copy, l=V("su", 80, 88))
+            if h >= HC:
+                act(V("hc", 128 * h, 128 * h + 128), V("HT"), AF.Copy, l=V("su", 72 + 8 * h, 80 + 8 * h))
             else:
                 copy(V("hc", 0, 128), V("HT"), l=V("su", 72, 80))
             dscan(V("tsb", 128 * h, 128 * h + 128), V("hc", 128 * h, 128 * h + 128), V("dL2", 0, 128))
@@ -601,23 +681,21 @@ def rank_program(g, core, T, topo):
             dma("s", T.ol[:, :], T.out[0:128:16, :], [V("out")], [])
         X = "X%d" % ((t + 1) % 2)
         for b in (0, 3, 1, 2):
-            o = ("pst", "ps1", "ps0", "psr")[b]
-            mm(V(o, 0, 128), V("wq", 128 * b, 128 * b + 128), V("wp", 128 * b, 128 * b + 128), V("lc%d" % t), V("ls%d" % t))
-            if b == 0:
-                ts(V("H", 0, 64), V(o, 0, 64), 0.0, 0.03125, OP.max, OP.mult)
+            o = ("psx", "ps1", "ps0", "psr")[b]
+            mm(V(o, 0, 128), V("wq", 128 * b, 128 * b + 128), V("wp", 128 * b, 128 * b + 128), V("Fq%d" % t, 64, 192), V("Fs%d" % t, 64, 192))
+            if b < HV:
+                ts(V("H", 64 * b, 64 * b + 64), V(o, 64, 128), 0.0, 0.03125, OP.max, OP.mult)
             else:
-                act(V("H", 64 * b, 64 * b + 64), V(o, 0, 64), AF.Relu, scale=0.03125)
-        for h in range(2):
-            hl = V("su", 24 + 8 * h, 32 + 8 * h)
-            for b in (0, 1, 3, 2) if h == 0 else (0, 3, 2, 1):
-                o = 256 * b + 128 * h
-                x = V(X, 512 * h + b, 512 * h + 512, 4)
-                if b < 2 - h:
-                    tt(x, V("H", 64 * b, 64 * b + 64), Tf(b, 128 * h, 128 * h + 128), OP.add, l=hl)
-                else:
-                    k = 512 if b == 1 else o - 512
-                    act(V("G3", k, k + 128), V("H", 64 * b, 64 * b + 64), AF.Copy, l=hl)
-                    tt(x, V("pst", 512 * b + 128 * h, 512 * b + 128 * h + 128), V("G3", k, k + 128), OP.add)
+                act(V("H", 64 * b, 64 * b + 64), V(o, 64, 128), AF.Relu, scale=0.03125)
+        for b, a, e, q in PICKS:
+            hl, x = V("su", 24 + a // 16, 24 + e // 16), V(X, 4 * a + b, 4 * e, 4)
+            if q == "v":
+                tt(x, V("H", 64 * b, 64 * b + 64), Tf(b, a, e), OP.add, l=hl)
+            else:
+                act(V("G3", 256 * b + a, 256 * b + e), V("H", 64 * b, 64 * b + 64), AF.Copy, l=hl)
+                for h in range(a, e, 128):
+                    tt(V(X, 4 * h + b, 4 * min(e, h + 128), 4), V("pst", 512 * b + h, 512 * b + min(e, h + 128)),
+                       V("G3", 256 * b + h, 256 * b + min(e, h + 128)), OP.add)
     product("vq", "vs", "X%d" % (R % 2), ("ps",))
     dma("a", T.oc[:, :], T.XQ[:, :].bitcast(dt.uint8), [XQ], [])
     for k in range(4):

import numpy as np
import math
from concourse.mybir import dt, AluOpType, AxisListType, ActivationFunctionType
import comms_topo

C, K, R = 256, 64, 3
STEP = [1, 2, 4]
F32, B16, I32, U16, U8, MX = "float32", "bfloat16", "int32", "uint16", "uint8", "float8_e4m3fn_x4"
EPS = 2.0 ** -19
LIFT, HUGE, ROUND = 2.0 ** 21, 2.0 ** 96, 3 * 2 ** 13
U = 128.0
BASE = 64.0 * U
CYCLE, FIXED, WAKE, NET, COPY = 0.83, 0.0, 230.0, 1600.0, 1800.0
CASES = ((1.0, 240.0, 1300.0), (1.0, 210.0, 2300.0), (1.3, 220.0, 1600.0))
TRIES, ALIKE, SEED, MOVES, HEAT = 300, 1.0, 0, 45000, 30.0
GT, HV, TM, HC = True, 1, True, 1
PICKS = ((0, 0, 128, "v"), (1, 0, 128, "v"), (2, 0, 128, "a"), (3, 0, 128, "a"), (0, 128, 256, "v"), (1, 128, 256, "a"), (2, 128, 256, "a"),
         (3, 128, 256, "a"))
NV, NS = 2, 5
ORDERS = {}

_SB = {
    F32: {"sm": 64, "c8": 8, "Sw": 776, "M": 128, "VV": 128, "PK": 128, "PKm": 128, "tmV": 256,
          "tmM": 128, "tmN": 128, "tsV": 256, "tsM": 128, "tsN": 128, "tR": 288, "d8": 8, "s8": 8, "tNP": 128, "NJ": 128, "nkL": 136, "nkR": 136, "RP0": 464, "RP1": 400, "RP2": 336, "RP3": 272,
          "np": 128, "s64": 64, "H": 256, "G3": 1024, "out": 256, "yb": 256, "ka": 128, "kc": 128, "fw": 64},
    B16: {"X0": 1024, "X1": 1024, "ut": 512, "vt": 512, "et": 520, "et1": 520, "rbt": 512, "one": 64, "idn": 128, "A": 272, "A2": 272,
          "du": 256, "hpx": 256, "hp": 128, "FV": 1024, "FE": 512, "UL": 1056, "ed": 416, "F": 512, "TU": 4096, "BI": 1024,
          "Ct": 144, "HT": 192, "colT": 320, "hc": 256, "NP0": 128, "NP1": 128},
    U16: {"su": 96},
    MX: {"uq0": 128, "uq": 128, "vq": 128, "wq": 512, "eq": 512, "rbq": 128, "FVq": 256, "FEq": 128, "XQ": 256},
    U8: {"us0": 128, "us": 128, "vs": 128, "wp": 512, "es": 512, "rbs": 128, "FVs": 256, "FEs": 128, "XS": 256},
}
for _t in range(R):
    for _n, _d in (("Fq", MX), ("Fs", U8)):
        _SB[_d]["%s%d" % (_n, _t)] = 192
_JOINT = {
    "kf": (F32, {"jc": 128, "cq": 8, "cw": 8, "b0": 4, "dX": 72}),
    "kb": (B16, {"mk": 256, "par": 256, "ng": 144, "mP": 128, "rst": 128, "mkV": 256, "rstV": 256, "dL": 64, "dL2": 128, "dL3": 256,
                 "mdL": 64, "mdL2": 128, "mdL3": 256, "edL": 64, "edL2": 128, "edL3": 256, "mt": 256, "pv": 256, "fv": 64}),
    "ki": (I32, {"c0": 8, "c1": 8, "c2": 8}),
    "eb": (B16, {"As": 128, "dA": 128, "npk": 256, "ni": 256, "mB": 258, "ph": 128, "fl": 64, "pf": 64, "fx": 64, "sv": 256, "nW": 256, "nW2": 256,
                 "d0": 256, "F1": 256, "u1": 256, "h1": 256, "t1": 256}),
    "rb": (B16, {"K": 128, "pK": 128, "Cm": 128, "Kc": 128, "y": 129, "bw": 128, "pen": 128, "bv": 128, "gl": 128, "vl": 128, "u2": 128,
                 "tsb": 256}),
}
WIDTH = {n: w for l in _SB.values() for n, w in l.items()}
TYPE = {n: d for d, l in _SB.items() for n in l}
PLACE = {}
SCRATCH = {n: ("sbuf", [128, WIDTH[n]], TYPE[n]) for n in WIDTH}
for _b, (_d, _l) in _JOINT.items():
    _o = 0
    for _n, _w in _l.items():
        PLACE[_n], WIDTH[_n], TYPE[_n] = (_b, _o), _w, _d
        _o += (_w + 31) // 32 * 32
    SCRATCH[_b] = ("sbuf", [128, _o], _d)
_PS = ("ps0", "ps1", "psr", "psx", "pst")
for _n in _PS:
    SCRATCH[_n] = ("psum", [128, 2048 if _n == "pst" else 512], F32)
    TYPE[_n] = F32
SEMAPHORES = ["qv", "qa", "qt", "qg"] + ["d%d" % i for i in range(40)] + ["%s%d%d" % (n, t, k) for n in ("arr", "snt") for t in range(R) for k in range(1)]


def planner(g, T):
    eng = {"v": g.vector, "a": g.scalar, "t": g.tensor, "g": g, "s": g.sync}
    ops, log, firsts, seen = [], {}, {}, {}

    def span(v):
        n, a, b, s = v
        if n in _PS:
            return n, a // 512 * 512, (b + 511) // 512 * 512, 1
        if s < 0:
            k = (a - b + (-s) - 1) // (-s)
            return n, a + s * (k - 1), a + 1, -s
        return n, a, b, s

    def meet(x, y):
        (_, a, b, s), (_, c, d, r) = x, y
        if a >= d or c >= b:
            return False
        return not (a - c) % math.gcd(s, r)

    def add(q, call, reads, writes, cost, hold=None, sem=None, inc=1, adds=False):
        i, pre = len(ops), {}
        for kind, vs in (("r", reads), ("w", writes)):
            for v in vs:
                x = span(v)
                for (y, k2, j) in log.get(x[0], []):
                    if meet(x, y) and (kind == "w" or k2 == "w" or (x[0] in _PS and ops[j]["q"] != q)):
                        pre[j] = pre.get(j, False) or not (adds and x[0] in _PS and ops[j]["q"] == q)
        for kind, vs in (("r", reads), ("w", writes)):
            for v in vs:
                x = span(v)
                l = log.setdefault(x[0], [])
                if kind == "w" and x[3] == 1:
                    l[:] = [e for e in l if not (x[1] <= e[0][1] and e[0][2] <= x[2])]
                l.append((x, kind, i))
        like = firsts.setdefault((q, str(writes or reads), seen.setdefault(str(writes or reads), [0])[0]), i)
        seen[str(writes or reads)][0] += 1
        ops.append({"q": q, "call": call, "pre": pre, "cost": cost, "hold": cost if hold is None else hold, "sem": sem or "q" + q, "inc": inc,
                    "like": like})

    def best_order():
        n = len(ops)
        succ, rank = [[] for _ in range(n)], [0.0] * n
        for i, o in enumerate(ops):
            for j, w in o["pre"].items():
                succ[j].append((i, WAKE if w else 0.0))
        for i in range(n - 1, -1, -1):
            rank[i] = ops[i]["cost"] + max([rank[k] + w for k, w in succ[i]], default=0.0)
        names = sorted({o["q"] for o in ops})
        qs = [names.index(o["q"]) for o in ops]
        cost, hold, need = [o["cost"] for o in ops], [o["hold"] for o in ops], [len(o["pre"]) for o in ops]

        def order(rk, patience):
            left, ready, free, cand = need[:], [0.0] * n, [0.0] * len(names), [[] for _ in names]
            pick, out, end = [None] * len(names), [], 0.0
            for i in range(n):
                if not left[i]:
                    cand[qs[i]].append(i)
            while True:
                best = None
                for q, l in enumerate(cand):
                    if not l:
                        continue
                    if pick[q] is None:
                        t = max(free[q], min([ready[i] for i in l])) + patience
                        top, r = -1, -1e18
                        for i in l:
                            if ready[i] <= t and rk[i] > r:
                                top, r = i, rk[i]
                        pick[q] = (max(free[q], ready[top]), -r, top)
                    if best is None or pick[q] < best[0]:
                        best = (pick[q], q)
                if best is None:
                    return end, out
                (t, _, i), q = best
                cand[q].remove(i)
                pick[q] = None
                out.append(i)
                free[q] = t + hold[i]
                done = t + cost[i]
                end = max(end, done)
                for k, w in succ[i]:
                    ready[k] = max(ready[k], done + w)
                    left[k] -= 1
                    if not left[k]:
                        cand[qs[k]].append(k)
                        pick[qs[k]] = None

        cases = []
        for f, wake, net in CASES:
            pre = [[(j, wake if w else 0.0) for j, w in o["pre"].items()] for o in ops]
            sent = [o["cost"] == NET for o in ops]
            c = [net if s else x if x > 1200.0 else f * x for s, x in zip(sent, cost)]
            cases.append((pre, c, [h if x > 1200.0 else f * h for x, h in zip(cost, hold)]))

        def judge(out):
            total = 0.0
            for pre, c, h in cases:
                fin, free, end = [0.0] * n, [0.0] * len(names), 0.0
                for i in out:
                    q = qs[i]
                    t = free[q]
                    for j, w in pre[i]:
                        x = fin[j] + w
                        if x > t:
                            t = x
                    free[q] = t + h[i]
                    fin[i] = t = t + c[i]
                    if t > end:
                        end = t
                total += end
            return total

        rng, best, least = np.random.default_rng(SEED), None, 1e18
        alike = np.array([o["like"] for o in ops])
        for k in range(TRIES):
            at = alike if k < TRIES * ALIKE else np.arange(n)
            if k < 100:
                noise, patience = (rng.random(n) * (0.0, 100.0, 300.0, 800.0)[k // 4 % 4])[at], (0.0, 20.0, 50.0, 100.0)[k % 4]
            else:
                noise, patience = best[2].copy(), best[3] if k % 5 else 10.0 * (k // 5 % 11)
                some = (np.abs(np.arange(n) - at[rng.integers(0, n)]) < (3, 10, 30, 100)[k % 4]) & (rng.random(n) < (0.6, 0.3, 0.15, 0.1)[k % 4])
                noise += (some * rng.normal(0.0, (100.0, 300.0, 800.0)[k % 3], n))[at]
            end, out = order([r + x for r, x in zip(rank, noise.tolist())], patience)
            if end > least + 500.0:
                continue
            least, end = min(least, end), judge(out)
            if best is None or end <= best[0]:
                best = (end, out, noise, patience)

        (p0, c0, h0), (p1, c1, h1), (p2, c2, h2) = cases
        edges = [[(j, a[1], b[1], c[1]) for (j, a, b, c) in zip([x[0] for x in p0[i]], p0[i], p1[i], p2[i])] for i in range(n)]
        after = [[k for k, w in succ[i]] for i in range(n)]
        twins = {}
        for i, o in enumerate(ops):
            twins.setdefault(o["like"], []).append(i)
        turn = {i: k for l in twins.values() for k, i in enumerate(l)}

        def run(lines):
            left, nxt = need[:], [-1] * n
            for l in lines:
                for a, b in zip(l, l[1:]):
                    nxt[a] = b
                    left[b] += 1
            s0, s1, s2, f0, f1, f2 = [0.0] * n, [0.0] * n, [0.0] * n, [0.0] * n, [0.0] * n, [0.0] * n
            out = [i for i in range(n) if not left[i]]
            for i in out:
                a, b, c = s0[i], s1[i], s2[i]
                for j, u, v, w in edges[i]:
                    x = f0[j] + u
                    if x > a:
                        a = x
                    x = f1[j] + v
                    if x > b:
                        b = x
                    x = f2[j] + w
                    if x > c:
                        c = x
                s0[i], s1[i], s2[i] = a, b, c
                f0[i], f1[i], f2[i] = a + c0[i], b + c1[i], c + c2[i]
                k = nxt[i]
                if k >= 0:
                    s0[k], s1[k], s2[k] = a + h0[i], b + h1[i], c + h2[i]
                    left[k] -= 1
                    if not left[k]:
                        out.append(k)
                for k in after[i]:
                    left[k] -= 1
                    if not left[k]:
                        out.append(k)
            if len(out) < n:
                return None
            return max(f0) + max(f1) + max(f2), out, ((s0, f0), (s1, f1), (s2, f2))

        def held(lines, times):
            prev, pairs = {b: a for l in lines for a, b in zip(l, l[1:])}, []
            for (s, f), (pre, c, h) in zip(times, cases):
                i = max(range(n), key=lambda x: f[x])
                while s[i] > 0.0:
                    j = next((j for j, w in pre[i] if f[j] + w >= s[i] - 1e-6), None)
                    if j is None:
                        j = prev[i]
                        pairs.append((j, i))
                    i = j
            return pairs

        lines = [[i for i in best[1] if qs[i] == q] for q in range(len(names))]
        now = top = run(lines)
        pairs = held(lines, now[2])
        for k in range(MOVES):
            j, i = pairs[int(rng.integers(len(pairs)))]
            far, back, both = int(rng.integers(1, 5)) if k % 2 else 1, k % 4 < 2, k % 3 and len(twins[ops[i]["like"]]) == len(twins[ops[j]["like"]])
            l = lines[qs[i]][:]
            for a, b in zip(twins[ops[j]["like"]], twins[ops[i]["like"]]) if both else [(j, i)]:
                x, y = l.index(a), l.index(b)
                if x < y and back:
                    l.insert(max(0, x - far + 1), l.pop(y))
                elif x < y:
                    l.insert(y + far - 1, l.pop(x))
            new = lines[:qs[i]] + [l] + lines[qs[i] + 1:]
            r = run(new)
            if r and r[0] <= now[0] + HEAT * (1.0 - k / MOVES) * rng.exponential():
                lines, now, pairs = new, r, held(new, r[2])
                if r[0] < top[0]:
                    top = r
        return top[1]

    def issue():
        key = str([(o["q"], o["cost"], sorted(o["pre"].items())) for o in ops])
        if key not in ORDERS:
            ORDERS[key] = best_order()
        count, at, known, snap = {}, {}, {q: {} for q in eng}, {}
        for i in ORDERS[key]:
            o = ops[i]
            q, s = o["q"], o["sem"]
            kn = known.setdefault(q, {})
            if q in eng:
                want = {}
                for j, w in o["pre"].items():
                    if w:
                        want[ops[j]["sem"]] = max(want.get(ops[j]["sem"], 0), at[j])
                for s2, m in sorted(want.items()):
                    if kn.get(s2, 0) >= m:
                        continue
                    eng[q].wait_ge(T.sem[s2], m)
                    kn[s2] = m
                    for k, x in snap.get((s2, m), {}).items():
                        kn[k] = max(kn.get(k, 0), x)
            count[s] = count.get(s, 0) + o["inc"]
            at[i] = count[s]
            if o["call"]:
                o["call"](eng[q])
            snap[(s, at[i])] = dict(kn) if q in eng else {}
        for s in sorted(count):
            if known["g"].get(s, 0) < count[s]:
                g.wait_ge(T.sem[s], count[s])
    return add, issue, seen


def rank_program(g, core, T, topo):
    rank = T.rank_of(core)
    if rank is None:
        return
    OP, AF = AluOpType, ActivationFunctionType
    add, issue, seen = planner(g, T)
    nd = [0]

    def V(n, a=None, b=None, s=1):
        if a is None:
            return (n, 0, WIDTH[n], 1)
        return (n, a, b, s)

    def ap(v):
        n, a, b, s = v
        if n in PLACE:
            n, o = PLACE[n]
            a, b = a + o, b + o
        if s < 0:
            return T[n][:, a:(b if b >= 0 else None):s]
        return T[n][:, a:b:s] if s != 1 else T[n][:, a:b]

    def ind(v, l):
        return ap(v).indirect(ap(l))

    def sc(x):
        return ap(x) if isinstance(x, tuple) else x

    def scr(*xs):
        return [x for x in xs if isinstance(x, tuple)]

    def width(v):
        return len(range(v[1], v[2], v[3]))

    def short(*vs):
        return all(TYPE[v[0]] in (B16, U16) for v in vs)

    def do(q, call, reads, writes, cycles, adds=False):
        add(q, lambda e: call(e).then_inc(T.sem["q" + q], 1), reads, writes, max(64, cycles) * CYCLE + FIXED, adds=adds)

    def dma(q, out, in_, reads, writes, cost=COPY):
        s = "d%d" % nd[0]
        nd[0] += 1
        add(q, lambda e: e.dma_start(out, in_).then_inc(T.sem[s], 16), reads, writes, cost, 100.0, s, 16)

    def tt(out, a, b, op, l=None):
        n = width(out)
        n = 60 + 1.5 * n if l else n if a[0] in _PS or b[0] in _PS else 2 * n
        do("v", lambda e: e.tensor_tensor(ap(out), ind(a, l) if l else ap(a), ap(b), op), [a, b] + scr(l), [out], n)

    def half(out, *a):
        return width(out) * (0.5 if short(out, *a) else 1.0)

    def ts(out, a, s1, s2, op0, op1=None):
        if op1 is None:
            do("v", lambda e: e.tensor_scalar(ap(out), ap(a), sc(s1), None, op0), [a] + scr(s1), [out], half(out, a))
        else:
            do("v", lambda e: e.tensor_scalar(ap(out), ap(a), sc(s1), sc(s2), op0, op1), [a] + scr(s1, s2), [out], half(out, a))

    def scan(out, d0, d1, init, op0, op1):
        do("v", lambda e: e.tensor_tensor_scan(ap(out), ap(d0), ap(d1), sc(init), op0, op1), [d0, d1] + scr(init), [out], half(out, d0, d1))

    def copy(out, a, l=None):
        do("v", lambda e: e.tensor_copy(ap(out), ind(a, l) if l else ap(a)), [a] + scr(l), [out], 60 + 1.5 * width(out) if l else half(out, a))

    def fill(v, c):
        do("v", lambda e: e.memset(ap(v), c), [], [v], half(v))

    def act(out, a, f, bias=0.0, scale=1.0, l=None, acc=None):
        def call(e):
            kw = {}
            if isinstance(bias, tuple) or bias != 0.0:
                kw["bias"] = sc(bias)
            if isinstance(scale, tuple) or scale != 1.0:
                kw["scale"] = sc(scale)
            if acc:
                kw["accum_out"] = ap(acc)
            return e.activation(ap(out), ind(a, l) if l else ap(a), f, **kw)
        n = width(out)
        do("a", call, [a] + scr(bias, scale, l), [out] + scr(acc), 78 + 1.5 * n if l else n + (24 if acc else 0))

    def quant(q, s, x):
        do("v", lambda e: e.quantize_mx(ap(q), ap(s), ap(x)), [x], [q, s], 14 + 0.265 * width(x))

    def mm(out, l, ls, r, rs, start=True, stop=True):
        do("t", lambda e: e.matmul_mx(ap(out), ap(l), ap(ls), ap(r), ap(rs), start, stop), [l, ls, r, rs], [out], width(r) + 16, not start)

    def iota(v, pat, base, cm):
        kw = {} if TYPE[v[0]] == I32 else {"allow_small_or_imprecise_dtypes": True}
        do("g", lambda e: e.iota(ap(v), pat, base, cm, **kw), [], [v], 160 + 2 * width(v))

    def level(n, a, b, c):
        iota(V(n, a, b), [[0, b - a]], c, 0)

    def select(v, pat, op, base, cm):
        do("g", lambda e: e.affine_select(ap(v), ap(v), pat, op, 0.0, base, cm), [v], [v], 200 + 2 * width(v))

    def bits(out, a, n):
        do("v", lambda e: e.tensor_scalar(ap(out), ap(a), n, None, OP.bitwise_and), [a], [out], width(out))

    def dscan(out, src, lift):
        scan(out, lift, src, 0.0, OP.add, OP.max)

    def less(out, a, b):
        scan(out, a, b, 0.0, OP.max, OP.subtract)

    LI, EL, NL, HL, UO = V("su", 0, 8), V("su", 8, 12), V("su", 16, 24), V("su", 24, 40), V("su", 40, 48)
    PL, N3, CL = V("su", 48, 56), V("su", 64, 72), V("su", 72, 88)

    dma("s", ap(V("X0")), T.x[:, :], [], [V("X0")], 1.4 * COPY)
    dma("a", ap(V("ut")), T.u[:, :], [], [V("ut")])
    dma("s", ap(V("wq")).bitcast(dt.uint8), T.wc[:, :], [V("X0"), V("ut")], [V("wq")])
    dma("s", ap(V("wp")), T.ws[:, :], [V("X0"), V("ut")], [V("wp")])
    dma("s", ap(V("vt")), T.v[:, :], [V("X0"), V("ut")], [V("vt")])

    iota(V("c1"), [[0, 8]], 0, 1)
    iota(V("mt"), [[0, 16], [1, 16]], 0, 0)
    bits(V("c2"), V("c1"), 15)
    copy(V("cq"), V("c2"))
    ts(V("mk"), V("mt"), V("cq", 0, 1), None, OP.is_equal)
    iota(V("c0"), [[16, 8]], 0, 0)
    copy(UO, V("c0"))
    for n, w, k, c0, c in (("par", 256, 2, 0.0, 1.0), ("rst", 128, 16, -4.95e29, 4.95e29), ("rstV", 256, 32, 4.95e29, -4.95e29)):
        fill(V(n, 0, w), c)
        fill(V(n, 0, w, k), c0)
    fill(V("Sw", 0, 8), -1e25)
    act(V("Sw", 264, 520), V("mt"), AF.Copy, scale=0.0, bias=-1e25)
    for p in range(2):
        ts(V("mkV", p, 256, 2), V("mk", 0, 128), 0.5, -9.9e29, OP.subtract, OP.mult)
    ts(V("tmV", 0, 1), V("mkV", 0, 1), -1e25, None, OP.max)
    act(V("mP"), V("mkV", 0, 256, 2), AF.Copy, scale=-1.0)
    for d, n, c0, c in (("dL", 64, -HUGE, LIFT), ("dL2", 128, -HUGE, 128.0 * U), ("dL3", 256, HUGE, -192.0)):
        act(V("m" + d), V("mk", 0, n), AF.Copy, scale=c0)
        fill(V("e" + d), c / c0)
        scan(V(d), V("e" + d), V("m" + d), 0.0, OP.mult, OP.add)
    fill(V("dX", 0, 36), 0.0)
    act(V("dX", 2, 34, 2), V("mk", 0, 16), AF.Copy, scale=-LIFT * EPS - 511.5 * EPS)
    tt(V("dX", 0, 32, 2), V("dX", 0, 32, 2), V("mdL3", 0, 16), OP.add)
    act(V("dX", 1, 33, 2), V("mk", 0, 16), AF.Copy, scale=1.0 + 512.0 * EPS)
    level("dX", 33, 34, -ROUND)
    level("dX", 34, 35, ROUND)
    act(V("dX", 36, 72), V("dX", 0, 36), AF.Copy)
    quant(V("uq0"), V("us0"), V("ut"))
    do("v", lambda e: e.tensor_copy(T.uq[:, 0:128].bitcast(dt.uint32), T.uq0[:, 0:128].bitcast(dt.uint32).indirect(ap(UO))), [V("uq0"), UO], [V("uq")], 250)
    act(V("us"), V("us0", 0, 128), AF.Copy, l=UO)
    fill(V("idn"), 1.0)
    fill(V("one"), 1.0)
    fill(V("c8"), 1024.0 * EPS)
    select(V("c8"), [[-16, 8]], OP.is_ge, 0, 1)
    select(V("c8"), [[16, 8]], OP.is_ge, 15, -1)
    for m in range(8):
        act(V("rbt", 64 * m, 64 * m + 64), V("one"), AF.Copy, scale=V("c8", m, m + 1))
    select(V("idn"), [[-1, 128]], OP.is_equal, 0, 1)
    iota(V("jc"), [[2, 128]], 131072, 0)
    act(V("jc"), V("jc"), AF.Copy, scale=EPS)
    iota(V("ng", 16, 144), [[-1, 128]], 128, 0)
    iota(V("pv"), [[1, 128], [0, 2]], 1, 0)
    iota(V("fv"), [[1, 64]], 129, 0)
    iota(V("b0"), [[24, 4]], 81, 0)
    iota(V("cw"), [[32, 8]], 0, 0)
    iota(V("HT", 128, 192), [[int(U), 64]], int(U), 0)
    iota(V("colT", 0, 256), [[1, 256]], -1, 0)
    iota(V("colT", 256, 320), [[1, 64]], 0, 0)
    for n, o in (("et", 4), ("et1", 5)):
        fill(V(n), 0.0)
        act(V(n, o, o + 509, 4), V("idn"), AF.Copy)
    for b in range(4):
        o = (4, 4, 2, 2)[b]
        quant(V("eq", 128 * b, 128 * b + 128), V("es", 128 * b, 128 * b + 128), V(("et", "et1")[b % 2], o, o + 512))
    quant(V("rbq"), V("rbs"), V("rbt"))
    for m in range(4):
        act(V("sm", m, m + 1), V("cq", 0, 1), AF.Copy, scale=U, bias=(16.0 * m + 0.5) * U + BASE)
    ts(V("sm", 11, 12), V("cq", 0, 1), 15.0, None, OP.is_lt)
    for k, c, c0 in ((8, LIFT, 129.0), (9, -128.0, -1.0), (13, 192.0, -1.0), (14, -LIFT, 127.0), (15, 96.0, 0.0)):
        act(V("sm", k, k + 1), V("sm", 11, 12), AF.Copy, scale=c, bias=c0)
    ts(V("sm", 15, 16), V("cq", 0, 1), V("sm", 15, 16), 2.0, OP.add, OP.mult)
    act(V("cw"), V("cw"), AF.Identity, bias=V("sm", 15, 16))
    for n, a, b, c in (("A", 256, 257, 0), ("nW", 0, 1, 1), ("UL", 15, 16, 1), ("UL", 1040, 1041, 1), ("nkL", 128, 129, 0), ("nkR", 128, 129, -1),
                       ("ng", 15, 16, 0), ("Ct", 0, 1, BASE), ("mB", 0, 2, 2 * U), ("y", 0, 1, U)):
        level(n, a, b, int(c))
    for h in range(4):
        level("RP%d" % h, 224, 264, 0)
    level("FE", 0, 512, 0)
    level("F", 256, 512, 0)
    quant(V("vq"), V("vs"), V("vt"))

    def send(t, k, pairs, cost):
        far = T.cores[rank ^ STEP[t]]
        rid, pid, _ = topo.addr(far)
        mask = topo.mask(core, T.cores[rank ^ STEP[-1]])
        n = len(pairs) * len(topo.engines(core, T.cores[rank ^ STEP[-1]]))
        arr, snt = "arr%d%d" % (t, k), "snt%d%d" % (t, k)

        def call(e):
            for a, b in pairs:
                a, b = [ap(x).bitcast(dt.uint8) if TYPE[x[0]] == MX else ap(x) for x in (a, b)]
                e.remote_dma(b, a, T.sem[arr], T.sem[snt], pid, rid, mask)
        add("g", call, [a for a, b in pairs], [], cost, 300.0 * len(pairs), snt, n)
        add("in", None, [a for a, b in pairs], [b for a, b in pairs], cost, 0.0, arr, n)

    XQ, XS, P = V("XQ"), V("XS"), V("psr", 0, 128)
    Cn = V("Ct", 1, 129)

    def product(l, ls, X, banks):
        for h in range(2):
            q, s = V("XQ", 128 * h, 128 * h + 128), V("XS", 128 * h, 128 * h + 128)
            quant(q, s, V(X, 512 * h, 512 * h + 512))
            for n in banks:
                n, o = ("ps%d" % h, 0) if n == "ps" else (n, 512 * h)
                mm(V(n, o, o + 128), V(l), V(ls), q, s)

    def ranks(tiles):
        for i, h in enumerate(tiles):
            x, q, s = (V("FE"), V("FEq"), V("FEs")) if h == 2 else (V("FV", 512 * h, 512 * h + 512), V("FVq", 128 * h, 128 * h + 128),
                                                                    V("FVs", 128 * h, 128 * h + 128))
            quant(q, s, x)
            mm(P, V("rbq"), V("rbs"), q, s, i == 0, i == len(tiles) - 1)

    def slot(m, a=0, b=128):
        o = 512 * (m // 4) + m % 4
        return V("FV", o + 4 * a, 512 * (m // 4) + 4 * b, 4)

    def Tf(b, a=0, e=256):
        return V("TU", 1024 * b + 256 + a, 1024 * b + 256 + e)

    for t in range(R):
        seen.clear()
        product("uq", "us", "X%d" % (t % 2), ("ps", "pst"))
        for h in range(2):
            act(V("Sw", 128 * h + 8, 128 * h + 136), V("pst", 512 * h, 512 * h + 128), AF.Copy)
        for b in range(4):
            mm(V("pst", 512 * b, 512 * b + 256), V("eq", 128 * b, 128 * b + 128), V("es", 128 * b, 128 * b + 128), XQ, XS)
        for h in range(2):
            S, o, e = "ps%d" % h, 128 * h, 128 - h
            tt(V("VV", o // 2, o // 2 + 64), V(S, 0, 128, 2), V("Sw", o + 7, o + 135, 2), OP.min)
            if TM:
                tt(V("tmV", o + 1, o + 1 + e), V(S, 0, e), V("mkV", o + 1, o + 1 + e), OP.max)
                scan(V("tsV", o, o + 128), V("rstV", o, o + 128), V("tmV", o, o + 128), 0.0, OP.max, OP.min)
            elif h:
                scan(V("tmV", 128, 256), V("VV"), V("mP"), -4e29, OP.max, OP.min)
                scan(V("tsV", 1, 256, 2), V("rst"), V("tmV", 128, 256), 0.0, OP.min, OP.max)
            tt(V("M", o // 2, o // 2 + 64), V(S, 0, 128, 2), V("Sw", o + 9, o + 137, 2), OP.max)
            tt(V("A", o, o + 128), V(S, 0, 128), V("Sw", o + 7, o + 135), OP.is_gt)
        for h in range(2):
            o, e = 128 * h, 128 - h
            tt(V("nW", o + 1, o + 1 + e), V("ps%d" % h, 0, e), V("Sw", o + 10, o + 10 + e), OP.is_ge)
        for m in range(8):
            s = V("tsV", 32 * m + 31, 32 * m + 32)
            if m < NV:
                ts(slot(m), V("VV"), s, None, OP.is_lt)
            else:
                act(slot(m), V("VV"), AF.Sign, bias=s, scale=-1.0)
        scan(V("tmM"), V("M"), V("mP"), -4e29, OP.max, OP.min)
        scan(V("tsM"), V("rst"), V("tmM"), 0.0, OP.min, OP.max)
        dma("s", T.Sw[:, 520:776], T.Sw[:, 8:264], [V("Sw", 8, 264)], [V("Sw", 520, 776)])
        act(V("As"), V("A", 0, 256, 2), AF.Copy, scale=EPS)
        less(V("NJ"), V("As"), V("jc"))
        scan(V("dA"), V("dL3", 0, 128), V("A", 1, 256, 2), 0.0, OP.add, OP.min)
        tt(V("sm", 40, 48), V("dA", 15, 128, 16), V("cw"), OP.add)
        copy(PL, V("sm", 40, 48))
        act(V("sm", 48, 56), V("sm", 40, 48), AF.Copy, scale=EPS, bias=0.625 + 256.0 * EPS)
        for m in range(8):
            act(V("UL", 16 + 128 * m, 144 + 128 * m), V("M"), AF.Sign, bias=V("tsM", 16 * m + 15, 16 * m + 16), scale=-1.0)
        ranks((0, 1))
        tt(V("nkL", 0, 128), P, V("NJ"), OP.subtract)
        act(V("nkR", 0, 128), V("nkL", 0, 128), AF.Copy, bias=-1.0)
        act(V("A2", 0, 257), V("A", 0, 257), AF.Copy, bias=512.0, scale=256.0)
        less(V("du"), V("A2", 0, 256), V("A2", 1, 257))
        scan(V("hpx"), V("par"), V("du"), 0.0, OP.mult, OP.max)
        act(V("hp"), V("hpx", 1, 256, 2), AF.Copy, scale=8e26, bias=-1e27)
        scan(V("PK"), V("hp"), V("M"), 0.0, OP.add, OP.min)
        for b in range(4):
            act(Tf(b), V("pst", 512 * b, 512 * b + 256), AF.Copy)
            for a in (256, 512):
                dma("s", ap(Tf(b, a, a + 256)), ap(Tf(b)), [Tf(b)], [Tf(b, a, a + 256)])
            act(V("BI", 256 * b, 256 * b + 256, 2), Tf(b), AF.Copy, scale=0.5, l=PL)
        for m in range(7, -1, -1):
            k, o = 16 * m + 15 + (m == 0), 224 + 36 * (m % 2)
            scan(V("RP%d" % (m // 2), o - 2 * k + 1, o, 2), V("UL", 144 * m + 31 - k, 144 * m + 31), V("nkL", 16 * m + 16 - k, 16 * m + 16),
                 V("sm", 48 + m, 49 + m), OP.mult, OP.max)
        for m in range(8):
            a, e, o = 16 * m, 127 + m // 7, 192 + 36 * (m % 2)
            scan(V("RP%d" % (m // 2), o + 2 * (e - 1 - a), o - 1, -2), V("UL", 16 + 128 * m + e, 16 + 128 * m + a, -1), V("nkR", e, a, -1),
                 -0.25, OP.min, OP.max)
        for h in range(4):
            scan(V("tR", 72 * h, 72 * h + 72), V("dX"), V("RP%d" % h, 192, 264), 0.0, OP.add, OP.min)
        tt(V("d8"), V("tR", 32, 288, 36), V("tR", 34, 288, 36), OP.subtract)
        ts(LI, V("d8"), 1.0 / EPS, 511.5, OP.mult, OP.add)
        tt(V("np"), V("Sw", 8, 776), V("PK"), OP.subtract, l=LI)
        for b in range(4):
            act(V("BI", 256 * b + 1, 256 * b + 256, 2), Tf(b, 0, 768), AF.Copy, scale=0.5, l=LI)
            scan(V("TU", 1024 * b, 1024 * b + 256), V("par"), V("BI", 256 * b, 256 * b + 256), 0.0, OP.mult, OP.add)
        if GT:
            scan(V("PKm"), V("PK"), V("mkV", 0, 256, 2), 4e29, OP.min, OP.max)
            tt(V("tmN"), V("Sw", 8, 776), V("PKm"), OP.subtract, l=LI)
        else:
            scan(V("tmN"), V("np"), V("mP"), -4e29, OP.max, OP.min)
        scan(V("tsN", 127, -1, -1), V("rst"), V("tmN", 127, -1, -1), 0.0, OP.min, OP.max)
        for m in range(8):
            s = V("tsN", 16 * m, 16 * m + 1)
            if m < NS:
                act(slot(m, 16 * m, 128), V("np", 16 * m, 128), AF.Relu, bias=s, scale=-1.0)
                act(slot(m, 16 * m, 128), slot(m, 16 * m, 128), AF.Sign)
            else:
                ts(slot(m, 16 * m, 128), V("np", 16 * m, 128), s, None, OP.is_lt)
            if m:
                ts(slot(m, 0, 16 * m), V("np", 0, 16 * m), s, None, OP.is_le)
        tt(V("FE", 0, 512, 4), V("np"), V("tsN"), OP.is_equal)
        ranks((2, 1, 0))
        act(V("npk"), V("du"), AF.Relu)
        act(V("npk"), V("npk"), AF.Copy, scale=-U / 256.0, bias=U)
        scan(V("ni"), V("npk"), V("npk"), 0.0, OP.add, OP.max)
        act(V("sm", 10, 11), V("ni", 255, 256), AF.Relu, bias=-192.0 * U)
        act(V("sm", 12, 13), V("sm", 10, 11), AF.Copy, scale=1024.0 * EPS / U, bias=65.0 * 1024.0 * EPS)
        ts(V("mB", 2, 258), V("ni"), V("sm", 10, 11), 2.0 * U, OP.min, OP.add)
        less(V("ph"), V("mB", 2, 258, 2), V("mB", 0, 256, 2))
        less(V("fl"), V("mB", 2, 66), V("mB", 1, 65))
        act(V("pf"), V("fl"), AF.Copy, scale=-2.0, bias=256.0)
        less(V("fx"), V("fv"), V("pf"))
        dscan(V("fw"), V("fx"), V("dL"))
        act(V("sm", 20, 24), V("fw", 15, 64, 16), AF.Identity, bias=V("sm", 14, 15))
        ts(V("sm", 24, 28), V("sm", 20, 24), 128.0, None, OP.is_lt)
        tt(V("sm", 28, 32), V("sm", 20, 24), V("b0"), OP.max)
        for m in range(7, -1, -1):
            k, o = 16 * m + 15 + (m == 0), 80 + 16 * (m % 4)
            scan(V("NP%d" % (m // 4), o - k, o), V("UL", 144 * m + 31 - k, 144 * m + 31), V("ng", 16 * m + 31 - k, 16 * m + 31), 200.0, OP.mult,
                 OP.max)
        for h in range(2):
            dscan(V("tNP", 64 * h, 64 * h + 64), V("NP%d" % h, 64, 128), V("dL"))
        act(V("sm", 32, 40), V("tNP", 15, 128, 16), AF.Identity, scale=-1.0, bias=V("sm", 8, 9))
        copy(NL, V("sm", 32, 40))
        act(V("s8"), V("d8"), AF.Relu, scale=512.0 / EPS, bias=256.0 * 512.0)
        tt(V("sm", 56, 64), V("sm", 32, 40), V("s8"), OP.subtract)
        copy(N3, V("sm", 56, 64))
        less(V("sv"), V("pv"), V("npk"))
        tt(V("sv", 0, 64), V("sv", 0, 64), V("fx"), OP.max)
        act(V("nW2"), V("nW"), AF.Copy, bias=512.0, scale=256.0)
        less(V("d0"), V("nW2"), V("A2", 0, 256))
        scan(V("F1"), V("d0"), V("sv"), 0.0, OP.min, OP.max)
        act(V("u1"), V("F1"), AF.Copy, scale=-256.0, bias=256.0)
        scan(V("h1", 255, -1, -1), V("u1", 255, -1, -1), V("F1", 255, -1, -1), 0.0, OP.min, OP.max)
        scan(V("t1"), V("dL3"), V("h1"), 0.0, OP.add, OP.min)
        ts(CL, V("t1", 15, 256, 16), V("sm", 13, 14), None, OP.add)
        ts(V("K"), P, V("sm", 12, 13), U, OP.is_ge, OP.mult)
        scan(Cn, V("K"), V("ph"), BASE, OP.add, OP.add)
        for m in range(4):
            act(V("ed", 104 * m, 104 * m + 80 + 8 * m), V("Ct", 1 + 8 * m, 81 + 16 * m), AF.Sign, bias=V("sm", m, m + 1), scale=-1.0,
                acc=V("sm", 16 + m, 17 + m))
            ts(V("su", 8 + m, 9 + m), V("sm", 16 + m, 17 + m), V("sm", 24 + m, 25 + m), V("sm", 28 + m, 29 + m), OP.mult, OP.add)
        for b in range(4):
            if b % 2:
                act(V("F", b, 256, 4), V("TU", 1024 * b, 1024 * b + 320), AF.Copy, l=EL)
            else:
                copy(V("F", b, 256, 4), V("TU", 1024 * b, 1024 * b + 320), l=EL)
        quant(V("Fq%d" % t, 0, 128), V("Fs%d" % t, 0, 128), V("F"))
        send(t, 0, [(V(n % t, 0, 64), V(n % t, 128, 192)) for n in ("Fq%d", "Fs%d")], NET)
        scan(V("Cm"), V("K"), V("ph"), BASE - U, OP.add, OP.add)
        tt(V("y", 1, 129), V("Ct", 0, 129), V("Cm"), OP.subtract, l=NL)
        act(V("pK"), V("K"), AF.Copy, scale=-128.0, bias=128.0 * U)
        less(V("Kc"), Cn, V("pK"))
        tt(V("bw"), V("Ct", 0, 129), V("Kc"), OP.max, l=N3)
        ts(V("pen"), V("y", 1, 129), 256.0, BASE, OP.mult, OP.max)
        less(V("bv"), V("bw"), V("pen"))
        scan(V("ka"), V("y", 0, 128), V("nkL", 0, 128), 0.0, OP.min, OP.max)
        scan(V("kc", 127, -1, -1), V("nkL", 128, 0, -1), V("y", 128, 0, -1), 0.9, OP.max, OP.min)
        tt(V("gl"), V("kc"), V("ka"), OP.is_gt)
        scan(V("vl"), V("gl"), V("bv"), 0.0, OP.mult, OP.max)
        ts(V("u2"), V("vl"), 0.0, None, OP.is_equal)
        scan(V("HT", 127, -1, -1), V("u2", 127, -1, -1), V("vl", 127, -1, -1), 0.0, OP.mult, OP.add)
        for h in range(2):
            if h >= HC:
                act(V("hc", 128 * h, 128 * h + 128), V("HT"), AF.Copy, l=V("su", 72 + 8 * h, 80 + 8 * h))
            else:
                copy(V("hc", 0, 128), V("HT"), l=V("su", 72, 80))
            dscan(V("tsb", 128 * h, 128 * h + 128), V("hc", 128 * h, 128 * h + 128), V("dL2", 0, 128))
            ts(V("su", 24 + 8 * h, 32 + 8 * h), V("tsb", 128 * h + 15, 128 * h + 128, 16), 1.0 / U, V("sm", 9, 10), OP.mult, OP.add)
        if t == R - 1:
            tt(V("colT", 1, 256, 2), V("colT", 1, 256, 2), V("A", 1, 256, 2), OP.add)
            act(V("s64"), V("colT"), AF.Copy, l=EL)
            act(V("out"), V("s64"), AF.Copy, l=HL)
            dma("s", T.ol[:, :], T.out[0:128:16, :], [V("out")], [])
        X = "X%d" % ((t + 1) % 2)
        for b in (0, 3, 1, 2):
            o = ("psx", "ps1", "ps0", "psr")[b]
            mm(V(o, 0, 128), V("wq", 128 * b, 128 * b + 128), V("wp", 128 * b, 128 * b + 128), V("Fq%d" % t, 64, 192), V("Fs%d" % t, 64, 192))
            if b < HV:
                ts(V("H", 64 * b, 64 * b + 64), V(o, 64, 128), 0.0, 0.03125, OP.max, OP.mult)
            else:
                act(V("H", 64 * b, 64 * b + 64), V(o, 64, 128), AF.Relu, scale=0.03125)
        for b, a, e, q in PICKS:
            hl, x = V("su", 24 + a // 16, 24 + e // 16), V(X, 4 * a + b, 4 * e, 4)
            if q == "v":
                tt(x, V("H", 64 * b, 64 * b + 64), Tf(b, a, e), OP.add, l=hl)
            else:
                act(V("G3", 256 * b + a, 256 * b + e), V("H", 64 * b, 64 * b + 64), AF.Copy, l=hl)
                for h in range(a, e, 128):
                    tt(V(X, 4 * h + b, 4 * min(e, h + 128), 4), V("pst", 512 * b + h, 512 * b + min(e, h + 128)),
                       V("G3", 256 * b + h, 256 * b + min(e, h + 128)), OP.add)
    product("vq", "vs", "X%d" % (R % 2), ("ps",))
    dma("a", T.oc[:, :], T.XQ[:, :].bitcast(dt.uint8), [XQ], [])
    for k in range(4):
        dma("a" if k % 2 else "s", T.osc[4 * k:4 * k + 4, :], T.XS[32 * k:32 * k + 4, :], [XS], [])
    act(V("yb", 0, 128), V("ps0", 0, 128), AF.Copy)
    copy(V("yb", 128, 256), V("ps1", 0, 128))
    dma("s", T.y[:, :], T.yb[:, :], [V("yb")], [])
    issue()
